import numpy as np
import ml_dtypes


def mxq(x, axis, fmt="e4m3"):
    dtype, down = {"e4m3": (ml_dtypes.float8_e4m3fn, 7), "e5m2": (ml_dtypes.float8_e5m2, 14)}[fmt]
    v = np.moveaxis(np.asarray(x, np.float32).astype(ml_dtypes.bfloat16).astype(np.float64), axis, -1)
    blocks = v.reshape(v.shape[:-1] + (-1, 32))
    amax = np.abs(blocks).max(-1, keepdims=True)
    byte = np.maximum(np.where(amax > 0, np.frexp(amax)[1] - 1 + 127, 0) - down, 1)
    scale = np.exp2(byte - 127.0)
    codes = (blocks / scale).astype(np.float32).astype(dtype).astype(np.float64)
    return np.moveaxis((codes * scale).reshape(v.shape), -1, axis)


WIDE = False


def mx_kscale(k):
    if not WIDE:
        return np.ones(k)
    levels = np.array([10, -10, 5, -5, 0])
    if k % 512:
        return np.exp2(np.random.permutation(np.resize(levels, k // 32))).repeat(32)
    a = np.empty((k // 512, 16))
    for p in range(k // 512):
        a[p, :8] = np.random.permutation(np.resize(levels, 8))
        for g in range(8):
            far = levels[np.abs(levels - a[p, g]) >= 10]
            a[p, g + 8] = far[np.random.randint(len(far))]
    return np.exp2(a.ravel()).repeat(32)


def f64(x):
    return np.asarray(x).astype(np.float64)


def striped(idx):
    return np.tile(np.asarray(idx).reshape(-1, 16).T, (8, 1)).astype(np.uint16)


def unstriped(offs):
    return offs[:16].T.reshape(-1).astype(np.int64)


E2M1 = np.array([0.0, 0.5, 1.0, 1.5, 2.0, 3.0, 4.0, 6.0, -0.0, -0.5, -1.0, -1.5, -2.0, -3.0, -4.0, -6.0])


def pack_weight(w, fmt):
    k, n = w.shape
    w = f64(np.asarray(w, np.float32).astype(ml_dtypes.bfloat16)).reshape(k // 32, 32, n)
    amax = np.abs(w).max(1)
    if fmt == "e4m3":
        byte = np.frexp(amax)[1] - 1 + 127 - 7
    else:
        mant, ex = np.frexp(amax / 6.0)
        byte = np.where(mant > 0.5, ex, ex - 1) + 127
    byte = np.clip(np.where(amax > 0, byte, 1), 1, 254)
    scaled = (w * np.exp2(127.0 - byte)[:, None, :]).reshape(k, n).astype(np.float32)
    by_word = np.ascontiguousarray(scaled.reshape(k // 512, 128, 4, n).transpose(0, 1, 3, 2))
    if fmt == "e4m3":
        words = by_word.astype(ml_dtypes.float8_e4m3fn).view(np.uint8)
    else:
        c = by_word.astype(ml_dtypes.float4_e2m1fn).view(np.uint8) & 0xF
        words = (c[..., 0::2] | (c[..., 1::2] << 4)).reshape(k // 512, 128, 2 * n)
    return np.ascontiguousarray(words), np.ascontiguousarray(byte.astype(np.uint8).reshape(k // 512, 16, n))


def unpack_weight(words, scales, fmt):
    g, _, n = scales.shape
    words = np.ascontiguousarray(words).reshape(g, 128, n, -1)
    if fmt == "e4m3":
        vals = words.view(ml_dtypes.float8_e4m3fn).astype(np.float64)
    else:
        nib = np.empty((g, 128, n, 4), np.uint8)
        nib[..., 0::2] = words & 0xF
        nib[..., 1::2] = words >> 4
        vals = E2M1[nib]
    vals = vals * np.repeat(np.exp2(scales.astype(np.float64) - 127.0), 8, axis=1)[..., None]
    return vals.transpose(0, 1, 3, 2).reshape(g * 512, n)


def bf(x):
    return np.asarray(x, np.float32).astype(ml_dtypes.bfloat16)


def planes(Y):
    r, m = Y.shape
    b = f64(bf(Y)).reshape(r // 32, 32, m)
    amax = np.abs(b).max(1)
    byte = np.clip(np.where(amax > 0, np.frexp(amax)[1] - 1 + 127 - 7, 1), 1, 254)
    codes = (b * np.exp2(127.0 - byte)[:, None, :]).reshape(r, m).astype(np.float32).astype(ml_dtypes.float8_e4m3fn).view(np.uint8)
    words = codes.reshape(r // 512, 128, 4, m).transpose(0, 1, 3, 2)
    return np.ascontiguousarray(words), np.ascontiguousarray(byte.astype(np.uint8).reshape(r // 512, 16, m))


D, T, I, U, J, Q = 512, 2048, 512, 1024, 256, 512


def setup_inputs():
    n = np.random.standard_normal
    idx = np.random.permutation(T)[:I]
    idx2 = np.random.permutation(U)[:J]
    fd = mx_kscale(D)
    candp = pack_weight(n((D, T)) / fd[:, None], "e4m3")
    return {
        "query": (n((D, Q)) * 0.8 / np.sqrt(D) * fd[:, None]).astype(np.float32),
        "cand_words": candp[0],
        "cand_scales": candp[1],
        "other": (n((D, U)) / fd[:, None]).astype(np.float32),
        "rc": np.tile(0.3 * n(T), (128, 1)).astype(np.float32),
        "offs": striped(idx),
        "offs2": striped(idx2),
    }


def reference(query, cand_words, cand_scales, other, rc, offs, offs2):
    idx = unstriped(offs)
    idx2 = unstriped(offs2)
    candu = unpack_weight(cand_words, cand_scales, "e4m3")
    queryq = mxq(f64(query), 0, "e4m3")
    candidxg = candu[:, idx]
    a = queryq.T @ candidxg
    otherq = mxq(f64(other), 0, "e4m3")
    b = queryq.T @ otherq
    m = np.mean(b[:, idx2], axis=1, keepdims=True)
    y = 2.0 * a - m - f64(rc)[:1][:, idx]
    words, scales = planes(y)
    return y, words, scales

@@ -1,0 +1,197 @@
+from contextlib import ExitStack
+
+import concourse.mybir as mybir
+from concourse.masks import make_identity
+
+D, T, I, U, J, Q = 512, 2048, 512, 1024, 256, 512
+FLOPS = 2 * D * Q * (I + U)
+
+F32 = mybir.dt.float32
+BF16 = mybir.dt.bfloat16
+I32 = mybir.dt.int32
+U32 = mybir.dt.uint32
+U16 = mybir.dt.uint16
+U8 = mybir.dt.uint8
+FP8X4 = mybir.dt.float8_e4m3fn_x4
+ACT = mybir.ActivationFunctionType
+ALU = mybir.AluOpType
+
+P = 128
+PACK = 4
+CHUNK = 256
+HALF = I // 2
+RC_ROW = 64
+Q_SPLIT = 84
+
+
+def tile_attend_localscaling_pl_kernel(tc, query, cand_words, cand_scales, other, rc, offs, offs2, out_0, out_1, out_2):
+    nc = tc.nc
+    with ExitStack() as ctx:
+        keep = ctx.enter_context(tc.tile_pool(name="keep", bufs=1))
+        reuse = ctx.enter_context(tc.tile_pool(name="reuse", bufs=1))
+        psum_b = ctx.enter_context(tc.psum_pool(name="psum_b", bufs=4))
+        psum_a = ctx.enter_context(tc.psum_pool(name="psum_a", bufs=4))
+
+        idx = keep.tile([P, I // 16], U16, name="idx")
+        idx2 = keep.tile([P, J // 16], U16, name="idx2")
+        nc.sync.dma_start(idx[:], offs)
+
+        scale_rows = keep.tile([16, T // 4], I32, name="scale_rows", align_bytes=64)
+        nc.scalar.dma_start(scale_rows[:], cand_scales[0].bitcast(I32))
+        rc_in = keep.tile([P, T], F32, name="rc_in", align_bytes=64)
+        rc_part = slice(RC_ROW, RC_ROW + 1)
+        nc.scalar.dma_start(rc_in[rc_part, :], rc[0:1, :])
+
+        n_chunks = U // CHUNK
+        o_raws = []
+
+        def load_chunk(c):
+            o_raw = keep.tile([P, PACK, CHUNK], F32, name="o_raw%d" % c, align_bytes=64)
+            nc.sync.dma_start(o_raw[:], other[:, c * CHUNK : (c + 1) * CHUNK].rearrange("(p j) c -> p j c", j=PACK))
+            o_raws.append(o_raw)
+
+        load_chunk(0)
+        q_raw = keep.tile([P, PACK, Q], F32, name="q_raw", tag="odd", align_bytes=64)
+        nc.sync.dma_start(q_raw[:], query.rearrange("(p j) c -> p j c", j=PACK))
+        for c in range(1, n_chunks):
+            load_chunk(c)
+        word_pool = keep.tile([P, T], I32, name="word_pool", align_bytes=64)
+        nc.sync.dma_start(word_pool[:], cand_words[0].rearrange("p n t -> p (n t)").bitcast(I32))
+        nc.sync.dma_start(idx2[:], offs2)
+
+        scale_pool = keep.tile([P, T], U8, name="scale_pool", align_bytes=64)
+        rc_pool = reuse.tile([P, T], F32, name="rc_pool", align_bytes=64, offset=0)
+        nc.vector.memset(scale_pool[:].bitcast(I32), 0)
+        nc.vector.memset(rc_pool[:], 0.0)
+        ident = keep.tile([P, P], F32, name="ident")
+        make_identity(nc, ident[:])
+
+        nc.vector.tensor_copy(scale_pool[0:16, :].bitcast(I32), scale_rows[:])
+        nc.scalar.copy(rc_pool[rc_part, :], rc_in[rc_part, :])
+
+        picked_s = keep.tile([P, I], U8, name="picked_s", align_bytes=64)
+        nc.vector.tensor_copy(picked_s[:], scale_pool[:].indirect(idx[:]))
+        cand_s = keep.tile([P, I], U8, name="cand_s", align_bytes=64)
+        nc.vector.tensor_copy(cand_s[:].bitcast(I32), picked_s[:].bitcast(I32))
+        for g in range(1, 4):
+            nc.sync.dma_start(cand_s[32 * g : 32 * g + 4, :].bitcast(I32), picked_s[4 * g : 4 * g + 4, :].bitcast(I32))
+
+        def round_chunk(c, o_bf):
+            dst = o_bf[:].rearrange("p (c i) j -> p c j i", i=4)
+            src = o_raws[c][:].rearrange("p j (c i) -> p c j i", i=4)
+            if c == 1:
+                nc.scalar.copy(dst, src)
+            else:
+                nc.vector.tensor_copy(dst, src)
+
+        o_bf0 = keep.tile([P, CHUNK, PACK], BF16, name="o_bf0", align_bytes=64)
+        round_chunk(0, o_bf0)
+
+        rc_row = keep.tile([P, I], F32, name="rc_row", align_bytes=64)
+        nc.vector.tensor_copy(rc_row[:], rc_pool[:].indirect(idx[:]))
+        turned = psum_a.tile([P, PACK, P], F32, name="turned", tag="a")
+        for g in range(PACK):
+            nc.tensor.transpose(turned[:, g, :], rc_row[:, g * P : (g + 1) * P], ident[:])
+
+        q_bf = reuse.tile([P, PACK, P, PACK], BF16, name="q_bf", align_bytes=64, offset=0)
+        q_dst = q_bf[:].rearrange("p t m j -> p m j t")
+        q_src = q_raw[:].rearrange("p j (m t) -> p m j t", t=PACK)
+        nc.vector.tensor_scalar(q_dst[:, :Q_SPLIT], q_src[:, :Q_SPLIT], 2.0, None, ALU.mult)
+        nc.scalar.activation(q_dst[:, Q_SPLIT:], q_src[:, Q_SPLIT:], ACT.Copy, scale=2.0)
+        rc_col = keep.tile([P, PACK], F32, name="rc_col")
+        nc.scalar.copy(rc_col[:], turned[:, :, RC_ROW])
+
+        o_w0 = reuse.tile([P, CHUNK], U32, name="o_w0", align_bytes=64, offset=4096)
+        o_s0 = keep.tile([P, CHUNK], U8, name="o_s0", align_bytes=64)
+        nc.vector.quantize_mx(out=o_w0[:].bitcast(FP8X4), scales=o_s0[:], in_=o_bf0[:].rearrange("p c j -> p (c j)"))
+        q_w = keep.tile([P, Q], U32, name="q_w", align_bytes=64)
+        q_s = keep.tile([P, Q], U8, name="q_s", align_bytes=64)
+        nc.vector.quantize_mx(out=q_w[:].bitcast(FP8X4), scales=q_s[:], in_=q_bf[:].rearrange("p t m j -> p (t m j)"))
+
+        b_sb = [keep.tile([P, 2, U], F32, name="b_sb%d" % h, align_bytes=64) for h in range(2)]
+        for c in range(n_chunks):
+            if c == 0:
+                o_w, o_s = o_w0, o_s0
+            else:
+                if c == 2:
+                    o_bf = reuse.tile([P, CHUNK, PACK], BF16, name="o_bf2", align_bytes=64, offset=0)
+                else:
+                    o_bf = keep.tile([P, CHUNK, PACK], BF16, name="o_bf%d" % c, tag="odd", align_bytes=64)
+                round_chunk(c, o_bf)
+                o_w = keep.tile([P, CHUNK], U32, name="o_w%d" % c, align_bytes=64)
+                o_s = keep.tile([P, CHUNK], U8, name="o_s%d" % c, align_bytes=64)
+                nc.vector.quantize_mx(out=o_w[:].bitcast(FP8X4), scales=o_s[:], in_=o_bf[:].rearrange("p c j -> p (c j)"))
+            for h in range(2):
+                bank = psum_b.tile([P, 2, CHUNK], F32, name="bank_b%d_%d" % (c, h), tag="b")
+                for u in range(2):
+                    cols = slice((2 * h + u) * P, (2 * h + u + 1) * P)
+                    nc.tensor.matmul_mx(
+                        out=bank[:, u, :],
+                        lhsT=q_w[:, cols].bitcast(FP8X4),
+                        lhsT_scale=q_s[:, cols],
+                        rhs=o_w[:].bitcast(FP8X4),
+                        rhs_scale=o_s[:],
+                        start=True,
+                        stop=True,
+                    )
+                nc.scalar.activation(b_sb[h][:, :, c * CHUNK : (c + 1) * CHUNK], bank[:], ACT.Copy, scale=0.5)
+
+        spread = psum_a.tile([P, PACK, P], F32, name="spread", tag="a")
+        for g in range(PACK):
+            nc.tensor.transpose(spread[:, g, :], rc_col[:, g : g + 1].to_broadcast([P, P]), ident[:])
+        rc_all = keep.tile([P, I], F32, name="rc_all", align_bytes=64)
+        nc.scalar.copy(rc_all[:], spread[:].rearrange("p g i -> p (g i)"))
+
+        cand_w = keep.tile([P, I], U32, name="cand_w", tag="odd", align_bytes=64)
+        nc.vector.tensor_copy(cand_w[:], word_pool[:].bitcast(U32).indirect(idx[:]))
+
+        means = []
+        for t in range(PACK):
+            picked = keep.tile([P, J], F32, name="picked%d" % t, align_bytes=64)
+            nc.vector.tensor_copy(picked[:], b_sb[t // 2][:, t % 2, :].indirect(idx2[:]))
+            shares = keep.tile([P, J], F32, name="shares%d" % t, align_bytes=64)
+            mean = keep.tile([P, 1], F32, name="mean%d" % t)
+            nc.scalar.activation(shares[:], picked[:], ACT.Copy, scale=1.0 / J, accum_out=mean[:])
+            means.append(mean)
+
+        banks = []
+        for t in range(PACK):
+            bank = psum_a.tile([P, I], F32, name="bank_a%d" % t, tag="a")
+            cols = slice(t * P, (t + 1) * P)
+            nc.tensor.matmul_mx(
+                out=bank[:],
+                lhsT=q_w[:, cols].bitcast(FP8X4),
+                lhsT_scale=q_s[:, cols],
+                rhs=cand_w[:].bitcast(FP8X4),
+                rhs_scale=cand_s[:],
+                start=True,
+                stop=True,
+            )
+            banks.append(bank)
+
+        y_w = keep.tile([P, I], I32, name="y_w", align_bytes=64)
+        y_s = keep.tile([P, I], U8, name="y_s", align_bytes=64)
+        out_rows = out_0.rearrange("(p t) i -> p t i", t=PACK)
+        out_words = out_1[0].rearrange("p n t -> p (n t)").bitcast(I32)
+        for h in range(2):
+            cols = slice(h * HALF, (h + 1) * HALF)
+            y = keep.tile([P, PACK, HALF], F32, name="y%d" % h, align_bytes=64)
+            for t in range(PACK):
+                nc.vector.scalar_tensor_tensor(
+                    y[:, t, :], banks[t][:, cols], means[t][:], rc_all[:, cols], ALU.subtract, ALU.subtract
+                )
+            nc.sync.dma_start(out_rows[:, :, cols], y[:])
+            y_bf = keep.tile([P, HALF, PACK], BF16, name="y_bf%d" % h, align_bytes=64)
+            dst = y_bf[:].rearrange("p (c i) t -> p c t i", i=4)
+            src = y[:].rearrange("p t (c i) -> p c t i", i=4)
+            if h == 0:
+                nc.scalar.copy(dst, src)
+            else:
+                nc.vector.tensor_copy(dst, src)
+            nc.vector.quantize_mx(
+                out=y_w[:, cols].bitcast(FP8X4), scales=y_s[:, cols], in_=y_bf[:].rearrange("p c t -> p (c t)")
+            )
+            nc.sync.dma_start(out_words[:, cols], y_w[:, cols])
+        for r in range(4):
+            eng = nc.scalar if r % 2 == 0 else nc.sync
+            eng.dma_start(out_2[0, r:16:4, :].bitcast(I32), y_s[r:P:32, :].bitcast(I32))

@@ -18,10 +18,11 @@ ALU = mybir.AluOpType
 
 P = 128
 PACK = 4
-CHUNK = 256
+CHUNK = 512
 HALF = I // 2
 RC_ROW = 64
-Q_SPLIT = 84
+Q_SPLIT = 80
+O_SPLIT = 48
 
 
 def tile_attend_localscaling_pl_kernel(tc, query, cand_words, cand_scales, other, rc, offs, offs2, out_0, out_1, out_2):
@@ -36,11 +37,11 @@ def tile_attend_localscaling_pl_kernel(tc, query, cand_words, cand_scales, other
         idx2 = keep.tile([P, J // 16], U16, name="idx2")
         nc.sync.dma_start(idx[:], offs)
 
-        scale_rows = keep.tile([16, T // 4], I32, name="scale_rows", align_bytes=64)
-        nc.scalar.dma_start(scale_rows[:], cand_scales[0].bitcast(I32))
-        rc_in = keep.tile([P, T], F32, name="rc_in", align_bytes=64)
+        rc_in = keep.tile([P, T], F32, name="rc_in", tag="first", align_bytes=64)
         rc_part = slice(RC_ROW, RC_ROW + 1)
-        nc.scalar.dma_start(rc_in[rc_part, :], rc[0:1, :])
+        nc.sync.dma_start(rc_in[rc_part, :], rc[0:1, :])
+        scale_rows = keep.tile([16, T // 4], I32, name="scale_rows", align_bytes=64)
+        nc.sync.dma_start(scale_rows[:], cand_scales[0].bitcast(I32))
 
         n_chunks = U // CHUNK
         o_raws = []
@@ -51,23 +52,26 @@ def tile_attend_localscaling_pl_kernel(tc, query, cand_words, cand_scales, other
             o_raws.append(o_raw)
 
         load_chunk(0)
-        q_raw = keep.tile([P, PACK, Q], F32, name="q_raw", tag="odd", align_bytes=64)
+        q_raw = keep.tile([P, PACK, Q], F32, name="q_raw", align_bytes=64)
         nc.sync.dma_start(q_raw[:], query.rearrange("(p j) c -> p j c", j=PACK))
         for c in range(1, n_chunks):
             load_chunk(c)
-        word_pool = keep.tile([P, T], I32, name="word_pool", align_bytes=64)
+        word_pool = keep.tile([P, T], I32, name="word_pool", tag="words", align_bytes=64)
         nc.sync.dma_start(word_pool[:], cand_words[0].rearrange("p n t -> p (n t)").bitcast(I32))
         nc.sync.dma_start(idx2[:], offs2)
 
         scale_pool = keep.tile([P, T], U8, name="scale_pool", align_bytes=64)
         rc_pool = reuse.tile([P, T], F32, name="rc_pool", align_bytes=64, offset=0)
         nc.vector.memset(scale_pool[:].bitcast(I32), 0)
-        nc.vector.memset(rc_pool[:], 0.0)
+        nc.vector.memset(rc_pool[:, : T // 2], 0.0)
+        nc.gpsimd.memset(rc_pool[:, T // 2 :], 0.0)
         ident = keep.tile([P, P], F32, name="ident")
         make_identity(nc, ident[:])
+        warm = keep.tile([P, 1], F32, name="warm")
+        nc.scalar.activation(warm[:], rc_pool[:, 0:1], ACT.Copy)
 
         nc.vector.tensor_copy(scale_pool[0:16, :].bitcast(I32), scale_rows[:])
-        nc.scalar.copy(rc_pool[rc_part, :], rc_in[rc_part, :])
+        nc.scalar.activation(rc_pool[rc_part, :], rc_in[rc_part, :], ACT.Copy)
 
         picked_s = keep.tile([P, I], U8, name="picked_s", align_bytes=64)
         nc.vector.tensor_copy(picked_s[:], scale_pool[:].indirect(idx[:]))
@@ -79,12 +83,13 @@ def tile_attend_localscaling_pl_kernel(tc, query, cand_words, cand_scales, other
         def round_chunk(c, o_bf):
             dst = o_bf[:].rearrange("p (c i) j -> p c j i", i=4)
             src = o_raws[c][:].rearrange("p j (c i) -> p c j i", i=4)
-            if c == 1:
-                nc.scalar.copy(dst, src)
+            if c == 0:
+                nc.vector.tensor_copy(dst[:, :O_SPLIT], src[:, :O_SPLIT])
+                nc.scalar.copy(dst[:, O_SPLIT:], src[:, O_SPLIT:])
             else:
                 nc.vector.tensor_copy(dst, src)
 
-        o_bf0 = keep.tile([P, CHUNK, PACK], BF16, name="o_bf0", align_bytes=64)
+        o_bf0 = keep.tile([P, CHUNK, PACK], BF16, name="o_bf0", tag="first", align_bytes=64)
         round_chunk(0, o_bf0)
 
         rc_row = keep.tile([P, I], F32, name="rc_row", align_bytes=64)
@@ -101,57 +106,57 @@ def tile_attend_localscaling_pl_kernel(tc, query, cand_words, cand_scales, other
         rc_col = keep.tile([P, PACK], F32, name="rc_col")
         nc.scalar.copy(rc_col[:], turned[:, :, RC_ROW])
 
-        o_w0 = reuse.tile([P, CHUNK], U32, name="o_w0", align_bytes=64, offset=4096)
-        o_s0 = keep.tile([P, CHUNK], U8, name="o_s0", align_bytes=64)
-        nc.vector.quantize_mx(out=o_w0[:].bitcast(FP8X4), scales=o_s0[:], in_=o_bf0[:].rearrange("p c j -> p (c j)"))
-        q_w = keep.tile([P, Q], U32, name="q_w", align_bytes=64)
-        q_s = keep.tile([P, Q], U8, name="q_s", align_bytes=64)
-        nc.vector.quantize_mx(out=q_w[:].bitcast(FP8X4), scales=q_s[:], in_=q_bf[:].rearrange("p t m j -> p (t m j)"))
-
-        b_sb = [keep.tile([P, 2, U], F32, name="b_sb%d" % h, align_bytes=64) for h in range(2)]
-        for c in range(n_chunks):
-            if c == 0:
-                o_w, o_s = o_w0, o_s0
-            else:
-                if c == 2:
-                    o_bf = reuse.tile([P, CHUNK, PACK], BF16, name="o_bf2", align_bytes=64, offset=0)
-                else:
-                    o_bf = keep.tile([P, CHUNK, PACK], BF16, name="o_bf%d" % c, tag="odd", align_bytes=64)
-                round_chunk(c, o_bf)
-                o_w = keep.tile([P, CHUNK], U32, name="o_w%d" % c, align_bytes=64)
-                o_s = keep.tile([P, CHUNK], U8, name="o_s%d" % c, align_bytes=64)
-                nc.vector.quantize_mx(out=o_w[:].bitcast(FP8X4), scales=o_s[:], in_=o_bf[:].rearrange("p c j -> p (c j)"))
-            for h in range(2):
-                bank = psum_b.tile([P, 2, CHUNK], F32, name="bank_b%d_%d" % (c, h), tag="b")
-                for u in range(2):
-                    cols = slice((2 * h + u) * P, (2 * h + u + 1) * P)
-                    nc.tensor.matmul_mx(
-                        out=bank[:, u, :],
-                        lhsT=q_w[:, cols].bitcast(FP8X4),
-                        lhsT_scale=q_s[:, cols],
-                        rhs=o_w[:].bitcast(FP8X4),
-                        rhs_scale=o_s[:],
-                        start=True,
-                        stop=True,
-                    )
-                nc.scalar.activation(b_sb[h][:, :, c * CHUNK : (c + 1) * CHUNK], bank[:], ACT.Copy, scale=0.5)
-
         spread = psum_a.tile([P, PACK, P], F32, name="spread", tag="a")
         for g in range(PACK):
             nc.tensor.transpose(spread[:, g, :], rc_col[:, g : g + 1].to_broadcast([P, P]), ident[:])
         rc_all = keep.tile([P, I], F32, name="rc_all", align_bytes=64)
         nc.scalar.copy(rc_all[:], spread[:].rearrange("p g i -> p (g i)"))
 
-        cand_w = keep.tile([P, I], U32, name="cand_w", tag="odd", align_bytes=64)
+        o_w0 = reuse.tile([P, CHUNK], U32, name="o_w0", align_bytes=64, offset=4096)
+        o_s0 = keep.tile([P, CHUNK], U8, name="o_s0", align_bytes=64)
+        nc.vector.quantize_mx(out=o_w0[:].bitcast(FP8X4), scales=o_s0[:], in_=o_bf0[:].rearrange("p c j -> p (c j)"))
+        q_w = keep.tile([P, Q], U32, name="q_w", align_bytes=64)
+        q_s = keep.tile([P, Q], U8, name="q_s", align_bytes=64)
+        for t in range(PACK):
+            cols = slice(t * P, (t + 1) * P)
+            nc.vector.quantize_mx(
+                out=q_w[:, cols].bitcast(FP8X4), scales=q_s[:, cols], in_=q_bf[:, t].rearrange("p m j -> p (m j)")
+            )
+
+        b_sb = [keep.tile([P, U], F32, name="b_sb%d" % t, align_bytes=64) for t in range(PACK)]
+        for c in range(n_chunks):
+            if c == 0:
+                o_w, o_s = o_w0, o_s0
+            else:
+                o_bf = reuse.tile([P, CHUNK, PACK], BF16, name="o_bf1", align_bytes=64, offset=0)
+                round_chunk(c, o_bf)
+                o_w = keep.tile([P, CHUNK], U32, name="o_w%d" % c, align_bytes=64)
+                o_s = keep.tile([P, CHUNK], U8, name="o_s%d" % c, align_bytes=64)
+                nc.vector.quantize_mx(out=o_w[:].bitcast(FP8X4), scales=o_s[:], in_=o_bf[:].rearrange("p c j -> p (c j)"))
+            for t in range(PACK):
+                bank = psum_b.tile([P, CHUNK], F32, name="bank_b%d_%d" % (c, t), tag="b")
+                cols = slice(t * P, (t + 1) * P)
+                nc.tensor.matmul_mx(
+                    out=bank[:],
+                    lhsT=q_w[:, cols].bitcast(FP8X4),
+                    lhsT_scale=q_s[:, cols],
+                    rhs=o_w[:].bitcast(FP8X4),
+                    rhs_scale=o_s[:],
+                    start=True,
+                    stop=True,
+                )
+                nc.scalar.activation(b_sb[t][:, c * CHUNK : (c + 1) * CHUNK], bank[:], ACT.Copy, scale=0.5)
+
+        cand_w = reuse.tile([P, I], U32, name="cand_w", align_bytes=64, offset=0)
         nc.vector.tensor_copy(cand_w[:], word_pool[:].bitcast(U32).indirect(idx[:]))
 
+        picked = keep.tile([P, PACK, J], F32, name="picked", tag="words", align_bytes=64)
         means = []
         for t in range(PACK):
-            picked = keep.tile([P, J], F32, name="picked%d" % t, align_bytes=64)
-            nc.vector.tensor_copy(picked[:], b_sb[t // 2][:, t % 2, :].indirect(idx2[:]))
+            nc.vector.tensor_copy(picked[:, t, :], b_sb[t][:].indirect(idx2[:]))
             shares = keep.tile([P, J], F32, name="shares%d" % t, align_bytes=64)
             mean = keep.tile([P, 1], F32, name="mean%d" % t)
-            nc.scalar.activation(shares[:], picked[:], ACT.Copy, scale=1.0 / J, accum_out=mean[:])
+            nc.scalar.activation(shares[:], picked[:, t, :], ACT.Copy, scale=1.0 / J, accum_out=mean[:])
             means.append(mean)
 
         banks = []

@@ -18,11 +18,13 @@ ALU = mybir.AluOpType
 
 P = 128
 PACK = 4
-CHUNK = 512
 HALF = I // 2
 RC_ROW = 64
-Q_SPLIT = 80
-O_SPLIT = 48
+CHUNK = 256
+N_CHUNKS = U // CHUNK
+Q_SPLIT = 84
+O_SPLIT = (28, 42, 64, 64)
+Y_SPLIT = 36
 
 
 def tile_attend_localscaling_pl_kernel(tc, query, cand_words, cand_scales, other, rc, offs, offs2, out_0, out_1, out_2):
@@ -30,48 +32,40 @@ def tile_attend_localscaling_pl_kernel(tc, query, cand_words, cand_scales, other
     with ExitStack() as ctx:
         keep = ctx.enter_context(tc.tile_pool(name="keep", bufs=1))
         reuse = ctx.enter_context(tc.tile_pool(name="reuse", bufs=1))
-        psum_b = ctx.enter_context(tc.psum_pool(name="psum_b", bufs=4))
-        psum_a = ctx.enter_context(tc.psum_pool(name="psum_a", bufs=4))
+        psum = ctx.enter_context(tc.psum_pool(name="psum", bufs=1))
 
         idx = keep.tile([P, I // 16], U16, name="idx")
         idx2 = keep.tile([P, J // 16], U16, name="idx2")
         nc.sync.dma_start(idx[:], offs)
 
-        rc_in = keep.tile([P, T], F32, name="rc_in", tag="first", align_bytes=64)
-        rc_part = slice(RC_ROW, RC_ROW + 1)
-        nc.sync.dma_start(rc_in[rc_part, :], rc[0:1, :])
+        scale_pool = keep.tile([P, T], U8, name="scale_pool", align_bytes=64)
+        rc_pool = keep.tile([P, T], F32, name="rc_pool", align_bytes=64)
+        nc.vector.memset(rc_pool[:, : T // 2], 0.0)
+        nc.gpsimd.memset(rc_pool[:, T // 2 :], 0.0)
+        nc.vector.memset(scale_pool[:].bitcast(I32), 0)
         scale_rows = keep.tile([16, T // 4], I32, name="scale_rows", align_bytes=64)
         nc.sync.dma_start(scale_rows[:], cand_scales[0].bitcast(I32))
 
-        n_chunks = U // CHUNK
-        o_raws = []
-
-        def load_chunk(c):
-            o_raw = keep.tile([P, PACK, CHUNK], F32, name="o_raw%d" % c, align_bytes=64)
-            nc.sync.dma_start(o_raw[:], other[:, c * CHUNK : (c + 1) * CHUNK].rearrange("(p j) c -> p j c", j=PACK))
-            o_raws.append(o_raw)
-
-        load_chunk(0)
         q_raw = keep.tile([P, PACK, Q], F32, name="q_raw", align_bytes=64)
         nc.sync.dma_start(q_raw[:], query.rearrange("(p j) c -> p j c", j=PACK))
-        for c in range(1, n_chunks):
-            load_chunk(c)
+        o_raws = []
+        for c in range(N_CHUNKS):
+            o_raw = keep.tile([P, PACK, CHUNK], F32, name="o_raw%d" % c, tag="o_raw%d" % c, align_bytes=64)
+            nc.sync.dma_start(o_raw[:], other[:, c * CHUNK : (c + 1) * CHUNK].rearrange("(p j) c -> p j c", j=PACK))
+            o_raws.append(o_raw)
+            if c == 1:
+                nc.sync.dma_start(rc_pool[RC_ROW : RC_ROW + 1, :], rc[0:1, :])
         word_pool = keep.tile([P, T], I32, name="word_pool", tag="words", align_bytes=64)
         nc.sync.dma_start(word_pool[:], cand_words[0].rearrange("p n t -> p (n t)").bitcast(I32))
         nc.sync.dma_start(idx2[:], offs2)
 
-        scale_pool = keep.tile([P, T], U8, name="scale_pool", align_bytes=64)
-        rc_pool = reuse.tile([P, T], F32, name="rc_pool", align_bytes=64, offset=0)
-        nc.vector.memset(scale_pool[:].bitcast(I32), 0)
-        nc.vector.memset(rc_pool[:, : T // 2], 0.0)
-        nc.gpsimd.memset(rc_pool[:, T // 2 :], 0.0)
         ident = keep.tile([P, P], F32, name="ident")
         make_identity(nc, ident[:])
         warm = keep.tile([P, 1], F32, name="warm")
-        nc.scalar.activation(warm[:], rc_pool[:, 0:1], ACT.Copy)
+        nc.vector.memset(warm[:], 0.0)
+        nc.scalar.activation(warm[:], warm[:], ACT.Copy)
 
         nc.vector.tensor_copy(scale_pool[0:16, :].bitcast(I32), scale_rows[:])
-        nc.scalar.activation(rc_pool[rc_part, :], rc_in[rc_part, :], ACT.Copy)
 
         picked_s = keep.tile([P, I], U8, name="picked_s", align_bytes=64)
         nc.vector.tensor_copy(picked_s[:], scale_pool[:].indirect(idx[:]))
@@ -80,41 +74,29 @@ def tile_attend_localscaling_pl_kernel(tc, query, cand_words, cand_scales, other
         for g in range(1, 4):
             nc.sync.dma_start(cand_s[32 * g : 32 * g + 4, :].bitcast(I32), picked_s[4 * g : 4 * g + 4, :].bitcast(I32))
 
-        def round_chunk(c, o_bf):
-            dst = o_bf[:].rearrange("p (c i) j -> p c j i", i=4)
-            src = o_raws[c][:].rearrange("p j (c i) -> p c j i", i=4)
-            if c == 0:
-                nc.vector.tensor_copy(dst[:, :O_SPLIT], src[:, :O_SPLIT])
-                nc.scalar.copy(dst[:, O_SPLIT:], src[:, O_SPLIT:])
-            else:
-                nc.vector.tensor_copy(dst, src)
-
-        o_bf0 = keep.tile([P, CHUNK, PACK], BF16, name="o_bf0", tag="first", align_bytes=64)
-        round_chunk(0, o_bf0)
-
-        rc_row = keep.tile([P, I], F32, name="rc_row", align_bytes=64)
-        nc.vector.tensor_copy(rc_row[:], rc_pool[:].indirect(idx[:]))
-        turned = psum_a.tile([P, PACK, P], F32, name="turned", tag="a")
-        for g in range(PACK):
-            nc.tensor.transpose(turned[:, g, :], rc_row[:, g * P : (g + 1) * P], ident[:])
-
-        q_bf = reuse.tile([P, PACK, P, PACK], BF16, name="q_bf", align_bytes=64, offset=0)
+        q_bf = keep.tile([P, PACK, P, PACK], BF16, name="q_bf", align_bytes=64)
         q_dst = q_bf[:].rearrange("p t m j -> p m j t")
         q_src = q_raw[:].rearrange("p j (m t) -> p m j t", t=PACK)
         nc.vector.tensor_scalar(q_dst[:, :Q_SPLIT], q_src[:, :Q_SPLIT], 2.0, None, ALU.mult)
         nc.scalar.activation(q_dst[:, Q_SPLIT:], q_src[:, Q_SPLIT:], ACT.Copy, scale=2.0)
-        rc_col = keep.tile([P, PACK], F32, name="rc_col")
-        nc.scalar.copy(rc_col[:], turned[:, :, RC_ROW])
 
-        spread = psum_a.tile([P, PACK, P], F32, name="spread", tag="a")
-        for g in range(PACK):
-            nc.tensor.transpose(spread[:, g, :], rc_col[:, g : g + 1].to_broadcast([P, P]), ident[:])
-        rc_all = keep.tile([P, I], F32, name="rc_all", align_bytes=64)
-        nc.scalar.copy(rc_all[:], spread[:].rearrange("p g i -> p (g i)"))
+        def round_chunk(c):
+            o_bf = keep.tile([P, CHUNK, PACK], BF16, name="o_bf%d" % c, tag="o_bf%d" % c, align_bytes=64)
+            dst = o_bf[:].rearrange("p (c i) j -> p c j i", i=4)
+            src = o_raws[c][:].rearrange("p j (c i) -> p c j i", i=4)
+            split = O_SPLIT[c]
+            nc.vector.tensor_copy(dst[:, :split], src[:, :split])
+            if split < CHUNK // 4:
+                nc.scalar.copy(dst[:, split:], src[:, split:])
+            return o_bf
 
-        o_w0 = reuse.tile([P, CHUNK], U32, name="o_w0", align_bytes=64, offset=4096)
-        o_s0 = keep.tile([P, CHUNK], U8, name="o_s0", align_bytes=64)
-        nc.vector.quantize_mx(out=o_w0[:].bitcast(FP8X4), scales=o_s0[:], in_=o_bf0[:].rearrange("p c j -> p (c j)"))
+        def quantize_chunk(c, o_bf):
+            o_w = keep.tile([P, CHUNK], U32, name="o_w%d" % c, align_bytes=64)
+            o_s = keep.tile([P, CHUNK], U8, name="o_s%d" % c, align_bytes=64)
+            nc.vector.quantize_mx(out=o_w[:].bitcast(FP8X4), scales=o_s[:], in_=o_bf[:].rearrange("p c j -> p (c j)"))
+            return o_w, o_s
+
+        o_bf = round_chunk(0)
         q_w = keep.tile([P, Q], U32, name="q_w", align_bytes=64)
         q_s = keep.tile([P, Q], U8, name="q_s", align_bytes=64)
         for t in range(PACK):
@@ -123,21 +105,16 @@ def tile_attend_localscaling_pl_kernel(tc, query, cand_words, cand_scales, other
                 out=q_w[:, cols].bitcast(FP8X4), scales=q_s[:, cols], in_=q_bf[:, t].rearrange("p m j -> p (m j)")
             )
 
-        b_sb = [keep.tile([P, U], F32, name="b_sb%d" % t, align_bytes=64) for t in range(PACK)]
-        for c in range(n_chunks):
-            if c == 0:
-                o_w, o_s = o_w0, o_s0
-            else:
-                o_bf = reuse.tile([P, CHUNK, PACK], BF16, name="o_bf1", align_bytes=64, offset=0)
-                round_chunk(c, o_bf)
-                o_w = keep.tile([P, CHUNK], U32, name="o_w%d" % c, align_bytes=64)
-                o_s = keep.tile([P, CHUNK], U8, name="o_s%d" % c, align_bytes=64)
-                nc.vector.quantize_mx(out=o_w[:].bitcast(FP8X4), scales=o_s[:], in_=o_bf[:].rearrange("p c j -> p (c j)"))
-            for t in range(PACK):
-                bank = psum_b.tile([P, CHUNK], F32, name="bank_b%d_%d" % (c, t), tag="b")
-                cols = slice(t * P, (t + 1) * P)
+        b_sb = [
+            reuse.tile([P, 2, U], F32, name="b_sb%d" % k, align_bytes=64, offset=k * U * 8) for k in range(2)
+        ]
+
+        def product_b(c, k, o_w, o_s):
+            bank = psum.tile([P, 2, CHUNK], F32, name="bank_b%d_%d" % (c, k), tag="bank%d" % (2 * c + k))
+            for e in range(2):
+                cols = slice((2 * k + e) * P, (2 * k + e + 1) * P)
                 nc.tensor.matmul_mx(
-                    out=bank[:],
+                    out=bank[:, e, :],
                     lhsT=q_w[:, cols].bitcast(FP8X4),
                     lhsT_scale=q_s[:, cols],
                     rhs=o_w[:].bitcast(FP8X4),
@@ -145,45 +122,77 @@ def tile_attend_localscaling_pl_kernel(tc, query, cand_words, cand_scales, other
                     start=True,
                     stop=True,
                 )
-                nc.scalar.activation(b_sb[t][:, c * CHUNK : (c + 1) * CHUNK], bank[:], ACT.Copy, scale=0.5)
+            return bank
 
-        cand_w = reuse.tile([P, I], U32, name="cand_w", align_bytes=64, offset=0)
+        def empty_b(c, k, bank):
+            nc.scalar.activation(b_sb[k][:, :, c * CHUNK : (c + 1) * CHUNK], bank[:], ACT.Copy, scale=0.5)
+
+        late = []
+        for c in range(N_CHUNKS):
+            if c > 0:
+                o_bf = round_chunk(c)
+            o_w, o_s = quantize_chunk(c, o_bf)
+            banks = [product_b(c, k, o_w, o_s) for k in range(2)]
+            if c < N_CHUNKS - 2:
+                for k in range(2):
+                    empty_b(c, k, banks[k])
+            else:
+                late.append(banks)
+        for k in range(2):
+            for n in range(2):
+                empty_b(N_CHUNKS - 2 + n, k, late[n][k])
+
+        rc_row = keep.tile([P, I], F32, name="rc_row", tag="o_raw%d" % (N_CHUNKS - 1), align_bytes=64)
+        nc.vector.tensor_copy(rc_row[:], rc_pool[:].indirect(idx[:]))
+        cand_w = keep.tile([P, I], U32, name="cand_w", align_bytes=64)
         nc.vector.tensor_copy(cand_w[:], word_pool[:].bitcast(U32).indirect(idx[:]))
+        turned = psum.tile([P, PACK, P], F32, name="turned", tag="bank0")
+        for g in range(PACK):
+            nc.tensor.transpose(turned[:, g, :], rc_row[:, g * P : (g + 1) * P], ident[:])
+        rc_col = keep.tile([P, PACK], F32, name="rc_col")
+        nc.scalar.copy(rc_col[:], turned[:, :, RC_ROW])
+        spread = psum.tile([P, PACK, P], F32, name="spread", tag="bank1")
+        for g in range(PACK):
+            nc.tensor.transpose(spread[:, g, :], rc_col[:, g : g + 1].to_broadcast([P, P]), ident[:])
+        rc_all = keep.tile([P, I], F32, name="rc_all", align_bytes=64)
+        nc.scalar.copy(rc_all[:], spread[:].rearrange("p g i -> p (g i)"))
 
-        picked = keep.tile([P, PACK, J], F32, name="picked", tag="words", align_bytes=64)
         means = []
         for t in range(PACK):
-            nc.vector.tensor_copy(picked[:, t, :], b_sb[t][:].indirect(idx2[:]))
+            picked_t = keep.tile([P, J], F32, name="picked%d" % t, align_bytes=64)
+            picked = picked_t[:]
+            nc.vector.tensor_copy(picked, b_sb[t // 2][:, t % 2, :].indirect(idx2[:]))
             shares = keep.tile([P, J], F32, name="shares%d" % t, align_bytes=64)
             mean = keep.tile([P, 1], F32, name="mean%d" % t)
-            nc.scalar.activation(shares[:], picked[:, t, :], ACT.Copy, scale=1.0 / J, accum_out=mean[:])
+            nc.scalar.activation(shares[:], picked, ACT.Copy, scale=1.0 / J, accum_out=mean[:])
             means.append(mean)
-
-        banks = []
-        for t in range(PACK):
-            bank = psum_a.tile([P, I], F32, name="bank_a%d" % t, tag="a")
-            cols = slice(t * P, (t + 1) * P)
-            nc.tensor.matmul_mx(
-                out=bank[:],
-                lhsT=q_w[:, cols].bitcast(FP8X4),
-                lhsT_scale=q_s[:, cols],
-                rhs=cand_w[:].bitcast(FP8X4),
-                rhs_scale=cand_s[:],
-                start=True,
-                stop=True,
-            )
-            banks.append(bank)
 
         y_w = keep.tile([P, I], I32, name="y_w", align_bytes=64)
         y_s = keep.tile([P, I], U8, name="y_s", align_bytes=64)
         out_rows = out_0.rearrange("(p t) i -> p t i", t=PACK)
         out_words = out_1[0].rearrange("p n t -> p (n t)").bitcast(I32)
+        banks = {}
+        for h in range(2):
+            cols = slice(h * HALF, (h + 1) * HALF)
+            for t in range(PACK):
+                bank = psum.tile([P, HALF], F32, name="bank_a%d_%d" % (h, t), tag="bank%d" % ((2 + PACK * h + t) % 8))
+                rows = slice(t * P, (t + 1) * P)
+                nc.tensor.matmul_mx(
+                    out=bank[:],
+                    lhsT=q_w[:, rows].bitcast(FP8X4),
+                    lhsT_scale=q_s[:, rows],
+                    rhs=cand_w[:, cols].bitcast(FP8X4),
+                    rhs_scale=cand_s[:, cols],
+                    start=True,
+                    stop=True,
+                )
+                banks[(h, t)] = bank
         for h in range(2):
             cols = slice(h * HALF, (h + 1) * HALF)
             y = keep.tile([P, PACK, HALF], F32, name="y%d" % h, align_bytes=64)
             for t in range(PACK):
                 nc.vector.scalar_tensor_tensor(
-                    y[:, t, :], banks[t][:, cols], means[t][:], rc_all[:, cols], ALU.subtract, ALU.subtract
+                    y[:, t, :], banks[(h, t)][:], means[t][:], rc_all[:, cols], ALU.subtract, ALU.subtract
                 )
             nc.sync.dma_start(out_rows[:, :, cols], y[:])
             y_bf = keep.tile([P, HALF, PACK], BF16, name="y_bf%d" % h, align_bytes=64)
@@ -192,7 +201,8 @@ def tile_attend_localscaling_pl_kernel(tc, query, cand_words, cand_scales, other
             if h == 0:
                 nc.scalar.copy(dst, src)
             else:
-                nc.vector.tensor_copy(dst, src)
+                nc.vector.tensor_copy(dst[:, :Y_SPLIT], src[:, :Y_SPLIT])
+                nc.scalar.copy(dst[:, Y_SPLIT:], src[:, Y_SPLIT:])
             nc.vector.quantize_mx(
                 out=y_w[:, cols].bitcast(FP8X4), scales=y_s[:, cols], in_=y_bf[:].rearrange("p c t -> p (c t)")
             )

@@ -44,7 +44,7 @@ def tile_attend_localscaling_pl_kernel(tc, query, cand_words, cand_scales, other
         nc.gpsimd.memset(rc_pool[:, T // 2 :], 0.0)
         nc.vector.memset(scale_pool[:].bitcast(I32), 0)
         scale_rows = keep.tile([16, T // 4], I32, name="scale_rows", align_bytes=64)
-        nc.sync.dma_start(scale_rows[:], cand_scales[0].bitcast(I32))
+        nc.scalar.dma_start(scale_rows[:], cand_scales[0].bitcast(I32))
 
         q_raw = keep.tile([P, PACK, Q], F32, name="q_raw", align_bytes=64)
         nc.sync.dma_start(q_raw[:], query.rearrange("(p j) c -> p j c", j=PACK))
@@ -194,7 +194,8 @@ def tile_attend_localscaling_pl_kernel(tc, query, cand_words, cand_scales, other
                 nc.vector.scalar_tensor_tensor(
                     y[:, t, :], banks[(h, t)][:], means[t][:], rc_all[:, cols], ALU.subtract, ALU.subtract
                 )
-            nc.sync.dma_start(out_rows[:, :, cols], y[:])
+                if t % 2 == 1:
+                    nc.sync.dma_start(out_rows[:, t - 1 : t + 1, cols], y[:, t - 1 : t + 1, :])
             y_bf = keep.tile([P, HALF, PACK], BF16, name="y_bf%d" % h, align_bytes=64)
             dst = y_bf[:].rearrange("p (c i) t -> p c t i", i=4)
             src = y[:].rearrange("p t (c i) -> p c t i", i=4)

@@ -23,8 +23,9 @@ RC_ROW = 64
 CHUNK = 256
 N_CHUNKS = U // CHUNK
 Q_SPLIT = 84
-O_SPLIT = (28, 42, 64, 64)
-Y_SPLIT = 36
+SHARED = 2
+O_SPLIT = (28, 42, 32, 32)
+Y_SPLIT = 32
 
 
 def tile_attend_localscaling_pl_kernel(tc, query, cand_words, cand_scales, other, rc, offs, offs2, out_0, out_1, out_2):
@@ -38,6 +39,10 @@ def tile_attend_localscaling_pl_kernel(tc, query, cand_words, cand_scales, other
         idx2 = keep.tile([P, J // 16], U16, name="idx2")
         nc.sync.dma_start(idx[:], offs)
 
+        one = keep.tile([P, 1], F32, name="one")
+        two = keep.tile([P, 1], F32, name="two")
+        nc.vector.memset(one[:], 1.0)
+        nc.scalar.activation(two[:], one[:], ACT.Copy, scale=2.0)
         scale_pool = keep.tile([P, T], U8, name="scale_pool", align_bytes=64)
         rc_pool = keep.tile([P, T], F32, name="rc_pool", align_bytes=64)
         nc.vector.memset(rc_pool[:, : T // 2], 0.0)
@@ -61,9 +66,6 @@ def tile_attend_localscaling_pl_kernel(tc, query, cand_words, cand_scales, other
 
         ident = keep.tile([P, P], F32, name="ident")
         make_identity(nc, ident[:])
-        warm = keep.tile([P, 1], F32, name="warm")
-        nc.vector.memset(warm[:], 0.0)
-        nc.scalar.activation(warm[:], warm[:], ACT.Copy)
 
         nc.vector.tensor_copy(scale_pool[0:16, :].bitcast(I32), scale_rows[:])
 
@@ -77,8 +79,10 @@ def tile_attend_localscaling_pl_kernel(tc, query, cand_words, cand_scales, other
         q_bf = keep.tile([P, PACK, P, PACK], BF16, name="q_bf", align_bytes=64)
         q_dst = q_bf[:].rearrange("p t m j -> p m j t")
         q_src = q_raw[:].rearrange("p j (m t) -> p m j t", t=PACK)
-        nc.vector.tensor_scalar(q_dst[:, :Q_SPLIT], q_src[:, :Q_SPLIT], 2.0, None, ALU.mult)
-        nc.scalar.activation(q_dst[:, Q_SPLIT:], q_src[:, Q_SPLIT:], ACT.Copy, scale=2.0)
+        for k in range(2):
+            pair = slice(2 * k, 2 * k + 2)
+            nc.vector.tensor_scalar(q_dst[:, :Q_SPLIT, :, pair], q_src[:, :Q_SPLIT, :, pair], 2.0, None, ALU.mult)
+        nc.scalar.activation(q_dst[:, Q_SPLIT:], q_src[:, Q_SPLIT:], ACT.Copy, scale=two[:])
 
         def round_chunk(c):
             o_bf = keep.tile([P, CHUNK, PACK], BF16, name="o_bf%d" % c, tag="o_bf%d" % c, align_bytes=64)
@@ -86,14 +90,21 @@ def tile_attend_localscaling_pl_kernel(tc, query, cand_words, cand_scales, other
             src = o_raws[c][:].rearrange("p j (c i) -> p c j i", i=4)
             split = O_SPLIT[c]
             nc.vector.tensor_copy(dst[:, :split], src[:, :split])
-            if split < CHUNK // 4:
+            if c < SHARED:
                 nc.scalar.copy(dst[:, split:], src[:, split:])
+            else:
+                nc.vector.tensor_copy(dst[:, split:], src[:, split:])
             return o_bf
 
         def quantize_chunk(c, o_bf):
             o_w = keep.tile([P, CHUNK], U32, name="o_w%d" % c, align_bytes=64)
             o_s = keep.tile([P, CHUNK], U8, name="o_s%d" % c, align_bytes=64)
-            nc.vector.quantize_mx(out=o_w[:].bitcast(FP8X4), scales=o_s[:], in_=o_bf[:].rearrange("p c j -> p (c j)"))
+            parts = 1 if c < SHARED else 2
+            for n in range(parts):
+                cols = slice(n * CHUNK // parts, (n + 1) * CHUNK // parts)
+                nc.vector.quantize_mx(
+                    out=o_w[:, cols].bitcast(FP8X4), scales=o_s[:, cols], in_=o_bf[:, cols].rearrange("p c j -> p (c j)")
+                )
             return o_w, o_s
 
         o_bf = round_chunk(0)
@@ -204,9 +215,14 @@ def tile_attend_localscaling_pl_kernel(tc, query, cand_words, cand_scales, other
             else:
                 nc.vector.tensor_copy(dst[:, :Y_SPLIT], src[:, :Y_SPLIT])
                 nc.scalar.copy(dst[:, Y_SPLIT:], src[:, Y_SPLIT:])
-            nc.vector.quantize_mx(
-                out=y_w[:, cols].bitcast(FP8X4), scales=y_s[:, cols], in_=y_bf[:].rearrange("p c t -> p (c t)")
-            )
+            parts = ((0, HALF),) if h == 0 else ((HALF // 2, HALF), (0, HALF // 2))
+            for lo, hi in parts:
+                part = slice(h * HALF + lo, h * HALF + hi)
+                nc.vector.quantize_mx(
+                    out=y_w[:, part].bitcast(FP8X4),
+                    scales=y_s[:, part],
+                    in_=y_bf[:, lo:hi].rearrange("p c t -> p (c t)"),
+                )
             nc.sync.dma_start(out_words[:, cols], y_w[:, cols])
         for r in range(4):
             eng = nc.scalar if r % 2 == 0 else nc.sync

@@ -18,21 +18,20 @@ ALU = mybir.AluOpType
 
 P = 128
 PACK = 4
+BANKS = 8
+RUN = 4
 HALF = I // 2
-RC_ROW = 64
 CHUNK = 256
 N_CHUNKS = U // CHUNK
-Q_SPLIT = 84
 SHARED = 2
-O_SPLIT = (28, 42, 32, 32)
-Y_SPLIT = 32
+Q_SPLIT = 84
+RC_ROW = 64
 
 
 def tile_attend_localscaling_pl_kernel(tc, query, cand_words, cand_scales, other, rc, offs, offs2, out_0, out_1, out_2):
     nc = tc.nc
     with ExitStack() as ctx:
         keep = ctx.enter_context(tc.tile_pool(name="keep", bufs=1))
-        reuse = ctx.enter_context(tc.tile_pool(name="reuse", bufs=1))
         psum = ctx.enter_context(tc.psum_pool(name="psum", bufs=1))
 
         idx = keep.tile([P, I // 16], U16, name="idx")
@@ -43,6 +42,7 @@ def tile_attend_localscaling_pl_kernel(tc, query, cand_words, cand_scales, other
         two = keep.tile([P, 1], F32, name="two")
         nc.vector.memset(one[:], 1.0)
         nc.scalar.activation(two[:], one[:], ACT.Copy, scale=2.0)
+
         scale_pool = keep.tile([P, T], U8, name="scale_pool", align_bytes=64)
         rc_pool = keep.tile([P, T], F32, name="rc_pool", align_bytes=64)
         nc.vector.memset(rc_pool[:, : T // 2], 0.0)
@@ -58,9 +58,9 @@ def tile_attend_localscaling_pl_kernel(tc, query, cand_words, cand_scales, other
             o_raw = keep.tile([P, PACK, CHUNK], F32, name="o_raw%d" % c, tag="o_raw%d" % c, align_bytes=64)
             nc.sync.dma_start(o_raw[:], other[:, c * CHUNK : (c + 1) * CHUNK].rearrange("(p j) c -> p j c", j=PACK))
             o_raws.append(o_raw)
-            if c == 1:
+            if c == SHARED - 1:
                 nc.sync.dma_start(rc_pool[RC_ROW : RC_ROW + 1, :], rc[0:1, :])
-        word_pool = keep.tile([P, T], I32, name="word_pool", tag="words", align_bytes=64)
+        word_pool = keep.tile([P, T], I32, name="word_pool", align_bytes=64)
         nc.sync.dma_start(word_pool[:], cand_words[0].rearrange("p n t -> p (n t)").bitcast(I32))
         nc.sync.dma_start(idx2[:], offs2)
 
@@ -68,7 +68,6 @@ def tile_attend_localscaling_pl_kernel(tc, query, cand_words, cand_scales, other
         make_identity(nc, ident[:])
 
         nc.vector.tensor_copy(scale_pool[0:16, :].bitcast(I32), scale_rows[:])
-
         picked_s = keep.tile([P, I], U8, name="picked_s", align_bytes=64)
         nc.vector.tensor_copy(picked_s[:], scale_pool[:].indirect(idx[:]))
         cand_s = keep.tile([P, I], U8, name="cand_s", align_bytes=64)
@@ -85,23 +84,22 @@ def tile_attend_localscaling_pl_kernel(tc, query, cand_words, cand_scales, other
         nc.scalar.activation(q_dst[:, Q_SPLIT:], q_src[:, Q_SPLIT:], ACT.Copy, scale=two[:])
 
         def round_chunk(c):
-            o_bf = keep.tile([P, CHUNK, PACK], BF16, name="o_bf%d" % c, tag="o_bf%d" % c, align_bytes=64)
-            dst = o_bf[:].rearrange("p (c i) j -> p c j i", i=4)
-            src = o_raws[c][:].rearrange("p j (c i) -> p c j i", i=4)
-            split = O_SPLIT[c]
-            nc.vector.tensor_copy(dst[:, :split], src[:, :split])
+            o_bf = keep.tile([P, CHUNK, PACK], BF16, name="o_bf%d" % c, align_bytes=64)
+            dst = o_bf[:].rearrange("p (c i) j -> p c j i", i=RUN)
+            src = o_raws[c][:].rearrange("p j (c i) -> p c j i", i=RUN)
+            middle = CHUNK // RUN // 2
+            nc.vector.tensor_copy(dst[:, :middle], src[:, :middle])
             if c < SHARED:
-                nc.scalar.copy(dst[:, split:], src[:, split:])
+                nc.scalar.copy(dst[:, middle:], src[:, middle:])
             else:
-                nc.vector.tensor_copy(dst[:, split:], src[:, split:])
+                nc.vector.tensor_copy(dst[:, middle:], src[:, middle:])
             return o_bf
 
         def quantize_chunk(c, o_bf):
             o_w = keep.tile([P, CHUNK], U32, name="o_w%d" % c, align_bytes=64)
             o_s = keep.tile([P, CHUNK], U8, name="o_s%d" % c, align_bytes=64)
-            parts = 1 if c < SHARED else 2
-            for n in range(parts):
-                cols = slice(n * CHUNK // parts, (n + 1) * CHUNK // parts)
+            for n in ((1, 0) if c < SHARED else (0, 1)):
+                cols = slice(n * CHUNK // 2, (n + 1) * CHUNK // 2)
                 nc.vector.quantize_mx(
                     out=o_w[:, cols].bitcast(FP8X4), scales=o_s[:, cols], in_=o_bf[:, cols].rearrange("p c j -> p (c j)")
                 )
@@ -116,23 +114,24 @@ def tile_attend_localscaling_pl_kernel(tc, query, cand_words, cand_scales, other
                 out=q_w[:, cols].bitcast(FP8X4), scales=q_s[:, cols], in_=q_bf[:, t].rearrange("p m j -> p (m j)")
             )
 
-        b_sb = [
-            reuse.tile([P, 2, U], F32, name="b_sb%d" % k, align_bytes=64, offset=k * U * 8) for k in range(2)
-        ]
+        def product(out, t, words, scales):
+            cols = slice(t * P, (t + 1) * P)
+            nc.tensor.matmul_mx(
+                out=out,
+                lhsT=q_w[:, cols].bitcast(FP8X4),
+                lhsT_scale=q_s[:, cols],
+                rhs=words.bitcast(FP8X4),
+                rhs_scale=scales,
+                start=True,
+                stop=True,
+            )
+
+        b_sb = [keep.tile([P, 2, U], F32, name="b_sb%d" % k, align_bytes=64) for k in range(2)]
 
         def product_b(c, k, o_w, o_s):
             bank = psum.tile([P, 2, CHUNK], F32, name="bank_b%d_%d" % (c, k), tag="bank%d" % (2 * c + k))
             for e in range(2):
-                cols = slice((2 * k + e) * P, (2 * k + e + 1) * P)
-                nc.tensor.matmul_mx(
-                    out=bank[:, e, :],
-                    lhsT=q_w[:, cols].bitcast(FP8X4),
-                    lhsT_scale=q_s[:, cols],
-                    rhs=o_w[:].bitcast(FP8X4),
-                    rhs_scale=o_s[:],
-                    start=True,
-                    stop=True,
-                )
+                product(bank[:, e, :], 2 * k + e, o_w[:], o_s[:])
             return bank
 
         def empty_b(c, k, bank):
@@ -143,12 +142,12 @@ def tile_attend_localscaling_pl_kernel(tc, query, cand_words, cand_scales, other
             if c > 0:
                 o_bf = round_chunk(c)
             o_w, o_s = quantize_chunk(c, o_bf)
-            banks = [product_b(c, k, o_w, o_s) for k in range(2)]
+            banks_b = [product_b(c, k, o_w, o_s) for k in range(2)]
             if c < N_CHUNKS - 2:
                 for k in range(2):
-                    empty_b(c, k, banks[k])
+                    empty_b(c, k, banks_b[k])
             else:
-                late.append(banks)
+                late.append(banks_b)
         for k in range(2):
             for n in range(2):
                 empty_b(N_CHUNKS - 2 + n, k, late[n][k])
@@ -157,6 +156,7 @@ def tile_attend_localscaling_pl_kernel(tc, query, cand_words, cand_scales, other
         nc.vector.tensor_copy(rc_row[:], rc_pool[:].indirect(idx[:]))
         cand_w = keep.tile([P, I], U32, name="cand_w", align_bytes=64)
         nc.vector.tensor_copy(cand_w[:], word_pool[:].bitcast(U32).indirect(idx[:]))
+
         turned = psum.tile([P, PACK, P], F32, name="turned", tag="bank0")
         for g in range(PACK):
             nc.tensor.transpose(turned[:, g, :], rc_row[:, g * P : (g + 1) * P], ident[:])
@@ -170,52 +170,45 @@ def tile_attend_localscaling_pl_kernel(tc, query, cand_words, cand_scales, other
 
         means = []
         for t in range(PACK):
-            picked_t = keep.tile([P, J], F32, name="picked%d" % t, align_bytes=64)
-            picked = picked_t[:]
-            nc.vector.tensor_copy(picked, b_sb[t // 2][:, t % 2, :].indirect(idx2[:]))
+            picked_b = keep.tile([P, J], F32, name="picked_b%d" % t, align_bytes=64)
+            nc.vector.tensor_copy(picked_b[:], b_sb[t // 2][:, t % 2, :].indirect(idx2[:]))
             shares = keep.tile([P, J], F32, name="shares%d" % t, align_bytes=64)
             mean = keep.tile([P, 1], F32, name="mean%d" % t)
-            nc.scalar.activation(shares[:], picked, ACT.Copy, scale=1.0 / J, accum_out=mean[:])
+            nc.scalar.activation(shares[:], picked_b[:], ACT.Copy, scale=1.0 / J, accum_out=mean[:])
             means.append(mean)
 
         y_w = keep.tile([P, I], I32, name="y_w", align_bytes=64)
         y_s = keep.tile([P, I], U8, name="y_s", align_bytes=64)
         out_rows = out_0.rearrange("(p t) i -> p t i", t=PACK)
         out_words = out_1[0].rearrange("p n t -> p (n t)").bitcast(I32)
-        banks = {}
+        banks_a = {}
         for h in range(2):
             cols = slice(h * HALF, (h + 1) * HALF)
             for t in range(PACK):
-                bank = psum.tile([P, HALF], F32, name="bank_a%d_%d" % (h, t), tag="bank%d" % ((2 + PACK * h + t) % 8))
-                rows = slice(t * P, (t + 1) * P)
-                nc.tensor.matmul_mx(
-                    out=bank[:],
-                    lhsT=q_w[:, rows].bitcast(FP8X4),
-                    lhsT_scale=q_s[:, rows],
-                    rhs=cand_w[:, cols].bitcast(FP8X4),
-                    rhs_scale=cand_s[:, cols],
-                    start=True,
-                    stop=True,
-                )
-                banks[(h, t)] = bank
+                bank = psum.tile([P, HALF], F32, name="bank_a%d_%d" % (h, t), tag="bank%d" % ((2 + PACK * h + t) % BANKS))
+                product(bank[:], t, cand_w[:, cols], cand_s[:, cols])
+                banks_a[(h, t)] = bank
+
         for h in range(2):
             cols = slice(h * HALF, (h + 1) * HALF)
             y = keep.tile([P, PACK, HALF], F32, name="y%d" % h, align_bytes=64)
             for t in range(PACK):
                 nc.vector.scalar_tensor_tensor(
-                    y[:, t, :], banks[(h, t)][:], means[t][:], rc_all[:, cols], ALU.subtract, ALU.subtract
+                    y[:, t, :], banks_a[(h, t)][:], means[t][:], rc_all[:, cols], ALU.subtract, ALU.subtract
                 )
                 if t % 2 == 1:
                     nc.sync.dma_start(out_rows[:, t - 1 : t + 1, cols], y[:, t - 1 : t + 1, :])
             y_bf = keep.tile([P, HALF, PACK], BF16, name="y_bf%d" % h, align_bytes=64)
-            dst = y_bf[:].rearrange("p (c i) t -> p c t i", i=4)
-            src = y[:].rearrange("p t (c i) -> p c t i", i=4)
+            dst = y_bf[:].rearrange("p (c i) t -> p c t i", i=RUN)
+            src = y[:].rearrange("p t (c i) -> p c t i", i=RUN)
             if h == 0:
                 nc.scalar.copy(dst, src)
+                parts = ((0, HALF),)
             else:
-                nc.vector.tensor_copy(dst[:, :Y_SPLIT], src[:, :Y_SPLIT])
-                nc.scalar.copy(dst[:, Y_SPLIT:], src[:, Y_SPLIT:])
-            parts = ((0, HALF),) if h == 0 else ((HALF // 2, HALF), (0, HALF // 2))
+                middle = HALF // RUN // 2
+                nc.vector.tensor_copy(dst[:, :middle], src[:, :middle])
+                nc.scalar.copy(dst[:, middle:], src[:, middle:])
+                parts = ((HALF // 2, HALF), (0, HALF // 2))
             for lo, hi in parts:
                 part = slice(h * HALF + lo, h * HALF + hi)
                 nc.vector.quantize_mx(
@@ -224,6 +217,7 @@ def tile_attend_localscaling_pl_kernel(tc, query, cand_words, cand_scales, other
                     in_=y_bf[:, lo:hi].rearrange("p c t -> p (c t)"),
                 )
             nc.sync.dma_start(out_words[:, cols], y_w[:, cols])
+
         for r in range(4):
-            eng = nc.scalar if r % 2 == 0 else nc.sync
-            eng.dma_start(out_2[0, r:16:4, :].bitcast(I32), y_s[r:P:32, :].bitcast(I32))
+            queue = nc.scalar if r % 2 == 0 else nc.sync
+            queue.dma_start(out_2[0, r:16:4, :].bitcast(I32), y_s[r:P:32, :].bitcast(I32))

@@ -18,7 +18,7 @@ ALU = mybir.AluOpType
 
 P = 128
 PACK = 4
-BANKS = 8
+A_BANKS = (2, 3, 4, 5, 7, 6, 0, 1)
 RUN = 4
 HALF = I // 2
 CHUNK = 256
@@ -128,8 +128,8 @@ def tile_attend_localscaling_pl_kernel(tc, query, cand_words, cand_scales, other
 
         b_sb = [keep.tile([P, 2, U], F32, name="b_sb%d" % k, align_bytes=64) for k in range(2)]
 
-        def product_b(c, k, o_w, o_s):
-            bank = psum.tile([P, 2, CHUNK], F32, name="bank_b%d_%d" % (c, k), tag="bank%d" % (2 * c + k))
+        def product_b(c, k, o_w, o_s, number):
+            bank = psum.tile([P, 2, CHUNK], F32, name="bank_b%d_%d" % (c, k), tag="bank%d" % number)
             for e in range(2):
                 product(bank[:, e, :], 2 * k + e, o_w[:], o_s[:])
             return bank
@@ -142,15 +142,12 @@ def tile_attend_localscaling_pl_kernel(tc, query, cand_words, cand_scales, other
             if c > 0:
                 o_bf = round_chunk(c)
             o_w, o_s = quantize_chunk(c, o_bf)
-            banks_b = [product_b(c, k, o_w, o_s) for k in range(2)]
-            if c < N_CHUNKS - 2:
-                for k in range(2):
-                    empty_b(c, k, banks_b[k])
+            empty_b(c, 0, product_b(c, 0, o_w, o_s, 2 * c))
+            if c == N_CHUNKS - 2:
+                late = [o_w, o_s]
             else:
-                late.append(banks_b)
-        for k in range(2):
-            for n in range(2):
-                empty_b(N_CHUNKS - 2 + n, k, late[n][k])
+                empty_b(c, 1, product_b(c, 1, o_w, o_s, 2 * c + 1))
+        empty_b(N_CHUNKS - 2, 1, product_b(N_CHUNKS - 2, 1, late[0], late[1], 2 * N_CHUNKS - 2))
 
         rc_row = keep.tile([P, I], F32, name="rc_row", tag="o_raw%d" % (N_CHUNKS - 1), align_bytes=64)
         nc.vector.tensor_copy(rc_row[:], rc_pool[:].indirect(idx[:]))
@@ -185,7 +182,7 @@ def tile_attend_localscaling_pl_kernel(tc, query, cand_words, cand_scales, other
         for h in range(2):
             cols = slice(h * HALF, (h + 1) * HALF)
             for t in range(PACK):
-                bank = psum.tile([P, HALF], F32, name="bank_a%d_%d" % (h, t), tag="bank%d" % ((2 + PACK * h + t) % BANKS))
+                bank = psum.tile([P, HALF], F32, name="bank_a%d_%d" % (h, t), tag="bank%d" % A_BANKS[PACK * h + t])
                 product(bank[:], t, cand_w[:, cols], cand_s[:, cols])
                 banks_a[(h, t)] = bank
 

@@ -18,7 +18,7 @@ ALU = mybir.AluOpType
 
 P = 128
 PACK = 4
-A_BANKS = (2, 3, 4, 5, 7, 6, 0, 1)
+A_BANKS = (0, 1, 2, 3, 4, 5, 6, 7)
 RUN = 4
 HALF = I // 2
 CHUNK = 256
@@ -60,9 +60,9 @@ def tile_attend_localscaling_pl_kernel(tc, query, cand_words, cand_scales, other
             o_raws.append(o_raw)
             if c == SHARED - 1:
                 nc.sync.dma_start(rc_pool[RC_ROW : RC_ROW + 1, :], rc[0:1, :])
+        nc.sync.dma_start(idx2[:], offs2)
         word_pool = keep.tile([P, T], I32, name="word_pool", align_bytes=64)
         nc.sync.dma_start(word_pool[:], cand_words[0].rearrange("p n t -> p (n t)").bitcast(I32))
-        nc.sync.dma_start(idx2[:], offs2)
 
         ident = keep.tile([P, P], F32, name="ident")
         make_identity(nc, ident[:])
@@ -128,45 +128,48 @@ def tile_attend_localscaling_pl_kernel(tc, query, cand_words, cand_scales, other
 
         b_sb = [keep.tile([P, 2, U], F32, name="b_sb%d" % k, align_bytes=64) for k in range(2)]
 
-        def product_b(c, k, o_w, o_s, number):
-            bank = psum.tile([P, 2, CHUNK], F32, name="bank_b%d_%d" % (c, k), tag="bank%d" % number)
-            for e in range(2):
-                product(bank[:, e, :], 2 * k + e, o_w[:], o_s[:])
-            return bank
+        quantized = []
 
-        def empty_b(c, k, bank):
-            nc.scalar.activation(b_sb[k][:, :, c * CHUNK : (c + 1) * CHUNK], bank[:], ACT.Copy, scale=0.5)
+        def fill_b(c, first, count, bank_number):
+            o_w, o_s = quantized[c]
+            bank = psum.tile([P, count, CHUNK], F32, name="bank_b%d_%d" % (c, first), tag="bank%d" % bank_number)
+            for e in range(count):
+                product(bank[:, e, :], first + e, o_w[:], o_s[:])
+            rows = slice(first % 2, first % 2 + count)
+            nc.scalar.activation(b_sb[first // 2][:, rows, c * CHUNK : (c + 1) * CHUNK], bank[:], ACT.Copy, scale=0.5)
 
-        late = []
         for c in range(N_CHUNKS):
             if c > 0:
                 o_bf = round_chunk(c)
-            o_w, o_s = quantize_chunk(c, o_bf)
-            empty_b(c, 0, product_b(c, 0, o_w, o_s, 2 * c))
-            if c == N_CHUNKS - 2:
-                late = [o_w, o_s]
-            else:
-                empty_b(c, 1, product_b(c, 1, o_w, o_s, 2 * c + 1))
-        empty_b(N_CHUNKS - 2, 1, product_b(N_CHUNKS - 2, 1, late[0], late[1], 2 * N_CHUNKS - 2))
-
+            quantized.append(quantize_chunk(c, o_bf))
+            if c < N_CHUNKS - 1:
+                fill_b(c, 0, 2, 2 * c)
+            if c < N_CHUNKS - 2:
+                fill_b(c, 2, 2, 2 * c + 1)
+        fill_b(3, 0, 1, 6)
+        fill_b(3, 1, 1, 7)
+        fill_b(3, 2, 2, 5)
         rc_row = keep.tile([P, I], F32, name="rc_row", tag="o_raw%d" % (N_CHUNKS - 1), align_bytes=64)
         nc.vector.tensor_copy(rc_row[:], rc_pool[:].indirect(idx[:]))
-        cand_w = keep.tile([P, I], U32, name="cand_w", align_bytes=64)
-        nc.vector.tensor_copy(cand_w[:], word_pool[:].bitcast(U32).indirect(idx[:]))
 
-        turned = psum.tile([P, PACK, P], F32, name="turned", tag="bank0")
+        turned = psum.tile([P, PACK, P], F32, name="turned", tag="bank4")
         for g in range(PACK):
             nc.tensor.transpose(turned[:, g, :], rc_row[:, g * P : (g + 1) * P], ident[:])
         rc_col = keep.tile([P, PACK], F32, name="rc_col")
         nc.scalar.copy(rc_col[:], turned[:, :, RC_ROW])
-        spread = psum.tile([P, PACK, P], F32, name="spread", tag="bank1")
+        spread = psum.tile([P, PACK, P], F32, name="spread", tag="bank7")
         for g in range(PACK):
             nc.tensor.transpose(spread[:, g, :], rc_col[:, g : g + 1].to_broadcast([P, P]), ident[:])
+        fill_b(2, 2, 2, 6)
+
         rc_all = keep.tile([P, I], F32, name="rc_all", align_bytes=64)
         nc.scalar.copy(rc_all[:], spread[:].rearrange("p g i -> p (g i)"))
 
         means = []
         for t in range(PACK):
+            if t == 2:
+                cand_w = keep.tile([P, I], U32, name="cand_w", align_bytes=64)
+                nc.vector.tensor_copy(cand_w[:], word_pool[:].bitcast(U32).indirect(idx[:]))
             picked_b = keep.tile([P, J], F32, name="picked_b%d" % t, align_bytes=64)
             nc.vector.tensor_copy(picked_b[:], b_sb[t // 2][:, t % 2, :].indirect(idx2[:]))
             shares = keep.tile([P, J], F32, name="shares%d" % t, align_bytes=64)

@@ -1,7 +1,6 @@
 from contextlib import ExitStack
 
 import concourse.mybir as mybir
-from concourse.masks import make_identity
 
 D, T, I, U, J, Q = 512, 2048, 512, 1024, 256, 512
 FLOPS = 2 * D * Q * (I + U)
@@ -18,14 +17,13 @@ ALU = mybir.AluOpType
 
 P = 128
 PACK = 4
-A_BANKS = (0, 1, 2, 3, 4, 5, 6, 7)
 RUN = 4
 HALF = I // 2
 CHUNK = 256
 N_CHUNKS = U // CHUNK
-SHARED = 2
 Q_SPLIT = 84
-RC_ROW = 64
+SHARED = 2
+RC_ROW = P - 1
 
 
 def tile_attend_localscaling_pl_kernel(tc, query, cand_words, cand_scales, other, rc, offs, offs2, out_0, out_1, out_2):
@@ -38,34 +36,42 @@ def tile_attend_localscaling_pl_kernel(tc, query, cand_words, cand_scales, other
         idx2 = keep.tile([P, J // 16], U16, name="idx2")
         nc.sync.dma_start(idx[:], offs)
 
-        one = keep.tile([P, 1], F32, name="one")
-        two = keep.tile([P, 1], F32, name="two")
-        nc.vector.memset(one[:], 1.0)
-        nc.scalar.activation(two[:], one[:], ACT.Copy, scale=2.0)
-
         scale_pool = keep.tile([P, T], U8, name="scale_pool", align_bytes=64)
         rc_pool = keep.tile([P, T], F32, name="rc_pool", align_bytes=64)
-        nc.vector.memset(rc_pool[:, : T // 2], 0.0)
-        nc.gpsimd.memset(rc_pool[:, T // 2 :], 0.0)
-        nc.vector.memset(scale_pool[:].bitcast(I32), 0)
+        nc.scalar.dma_start(rc_pool[RC_ROW : RC_ROW + 1, :], rc[0:1, :])
         scale_rows = keep.tile([16, T // 4], I32, name="scale_rows", align_bytes=64)
-        nc.scalar.dma_start(scale_rows[:], cand_scales[0].bitcast(I32))
+        nc.sync.dma_start(scale_rows[:], cand_scales[0].bitcast(I32))
 
-        q_raw = keep.tile([P, PACK, Q], F32, name="q_raw", align_bytes=64)
-        nc.sync.dma_start(q_raw[:], query.rearrange("(p j) c -> p j c", j=PACK))
-        o_raws = []
-        for c in range(N_CHUNKS):
-            o_raw = keep.tile([P, PACK, CHUNK], F32, name="o_raw%d" % c, tag="o_raw%d" % c, align_bytes=64)
-            nc.sync.dma_start(o_raw[:], other[:, c * CHUNK : (c + 1) * CHUNK].rearrange("(p j) c -> p j c", j=PACK))
-            o_raws.append(o_raw)
-            if c == SHARED - 1:
-                nc.sync.dma_start(rc_pool[RC_ROW : RC_ROW + 1, :], rc[0:1, :])
-        nc.sync.dma_start(idx2[:], offs2)
-        word_pool = keep.tile([P, T], I32, name="word_pool", align_bytes=64)
-        nc.sync.dma_start(word_pool[:], cand_words[0].rearrange("p n t -> p (n t)").bitcast(I32))
+        ones = keep.tile([P, 32], F32, name="ones", align_bytes=64)
+        two = keep.tile([P, 1], F32, name="two")
+        nc.vector.memset(ones[:], 1.0)
+        nc.scalar.activation(two[:], ones[:, 0:1], ACT.Copy, scale=2.0)
 
         ident = keep.tile([P, P], F32, name="ident")
-        make_identity(nc, ident[:])
+        ramp = keep.tile([P, 32], F32, name="ramp", align_bytes=64)
+        lane = keep.tile([P, 32], F32, name="lane", align_bytes=64)
+        nc.vector.memset(ident[:], 0.0)
+        nc.vector.tensor_tensor_scan(ramp[:], ones[:], ones[:], 0.0, ALU.mult, ALU.add)
+        nc.vector.memset(rc_pool[:RC_ROW, :].bitcast(I32), 0)
+        nc.vector.transpose(lane[:], ramp[:])
+        nc.vector.memset(scale_pool[:].bitcast(I32), 0)
+        for g in range(4):
+            rows = slice(32 * g, 32 * g + 32)
+            nc.vector.tensor_tensor(ident[rows, rows], ramp[rows, :], lane[rows, :], ALU.is_equal)
+
+        q_raw = keep.tile([P, PACK, Q], F32, name="q_raw", tag="q_raw", align_bytes=64)
+        nc.sync.dma_start(q_raw[:], query.rearrange("(p j) c -> p j c", j=PACK))
+        o_raws = []
+
+        def load_chunk(c):
+            o_raw = keep.tile([P, PACK, CHUNK], F32, name="o_raw%d" % c, align_bytes=64)
+            nc.sync.dma_start(o_raw[:], other[:, c * CHUNK : (c + 1) * CHUNK].rearrange("(p j) c -> p j c", j=PACK))
+            o_raws.append(o_raw)
+
+        for c in range(3):
+            load_chunk(c)
+        nc.sync.dma_start(idx2[:], offs2)
+
 
         nc.vector.tensor_copy(scale_pool[0:16, :].bitcast(I32), scale_rows[:])
         picked_s = keep.tile([P, I], U8, name="picked_s", align_bytes=64)
@@ -74,6 +80,16 @@ def tile_attend_localscaling_pl_kernel(tc, query, cand_words, cand_scales, other
         nc.vector.tensor_copy(cand_s[:].bitcast(I32), picked_s[:].bitcast(I32))
         for g in range(1, 4):
             nc.sync.dma_start(cand_s[32 * g : 32 * g + 4, :].bitcast(I32), picked_s[4 * g : 4 * g + 4, :].bitcast(I32))
+        for c in range(3, N_CHUNKS):
+            load_chunk(c)
+        word_pool = keep.tile([P, T], I32, name="word_pool", align_bytes=64)
+        nc.sync.dma_start(word_pool[:], cand_words[0].rearrange("p n t -> p (n t)").bitcast(I32))
+
+        rc_row = keep.tile([P, I], F32, name="rc_row", align_bytes=64)
+        nc.scalar.activation(rc_row[:], rc_pool[:].indirect(idx[:]), ACT.Copy)
+        turned = psum.tile([P, PACK, P], F32, name="turned", tag="bank6")
+        for g in range(PACK):
+            nc.tensor.transpose(turned[:, g, :], rc_row[:, g * P : (g + 1) * P], ident[:])
 
         q_bf = keep.tile([P, PACK, P, PACK], BF16, name="q_bf", align_bytes=64)
         q_dst = q_bf[:].rearrange("p t m j -> p m j t")
@@ -82,6 +98,12 @@ def tile_attend_localscaling_pl_kernel(tc, query, cand_words, cand_scales, other
             pair = slice(2 * k, 2 * k + 2)
             nc.vector.tensor_scalar(q_dst[:, :Q_SPLIT, :, pair], q_src[:, :Q_SPLIT, :, pair], 2.0, None, ALU.mult)
         nc.scalar.activation(q_dst[:, Q_SPLIT:], q_src[:, Q_SPLIT:], ACT.Copy, scale=two[:])
+
+        rc_col = keep.tile([P, PACK], F32, name="rc_col")
+        nc.scalar.copy(rc_col[:], turned[:, :, RC_ROW])
+        spread = psum.tile([P, PACK, P], F32, name="spread", tag="bank7")
+        for g in range(PACK):
+            nc.tensor.transpose(spread[:, g, :], rc_col[:, g : g + 1].to_broadcast([P, P]), ident[:])
 
         def round_chunk(c):
             o_bf = keep.tile([P, CHUNK, PACK], BF16, name="o_bf%d" % c, align_bytes=64)
@@ -114,6 +136,9 @@ def tile_attend_localscaling_pl_kernel(tc, query, cand_words, cand_scales, other
                 out=q_w[:, cols].bitcast(FP8X4), scales=q_s[:, cols], in_=q_bf[:, t].rearrange("p m j -> p (m j)")
             )
 
+        rc_all = keep.tile([P, I], F32, name="rc_all", align_bytes=64)
+        nc.scalar.copy(rc_all[:], spread[:].rearrange("p g i -> p (g i)"))
+
         def product(out, t, words, scales):
             cols = slice(t * P, (t + 1) * P)
             nc.tensor.matmul_mx(
@@ -126,95 +151,106 @@ def tile_attend_localscaling_pl_kernel(tc, query, cand_words, cand_scales, other
                 stop=True,
             )
 
-        b_sb = [keep.tile([P, 2, U], F32, name="b_sb%d" % k, align_bytes=64) for k in range(2)]
-
+        b_sb = keep.tile([P, PACK, U], F32, name="b_sb", align_bytes=64)
         quantized = []
 
-        def fill_b(c, first, count, bank_number):
-            o_w, o_s = quantized[c]
-            bank = psum.tile([P, count, CHUNK], F32, name="bank_b%d_%d" % (c, first), tag="bank%d" % bank_number)
-            for e in range(count):
-                product(bank[:, e, :], first + e, o_w[:], o_s[:])
-            rows = slice(first % 2, first % 2 + count)
-            nc.scalar.activation(b_sb[first // 2][:, rows, c * CHUNK : (c + 1) * CHUNK], bank[:], ACT.Copy, scale=0.5)
+        def fill_b(bank_number, tiles, chunks, on_vector):
+            bank = psum.tile([P, len(tiles), len(chunks), CHUNK], F32, name="bank_b%d" % bank_number, tag="bank%d" % bank_number)
+            for e, t in enumerate(tiles):
+                for n, c in enumerate(chunks):
+                    product(bank[:, e, n, :], t, quantized[c][0][:], quantized[c][1][:])
+            dst = b_sb[:, tiles[0] : tiles[-1] + 1, chunks[0] * CHUNK : (chunks[-1] + 1) * CHUNK]
+            src = bank[:].rearrange("p e n c -> p e (n c)")
+            if on_vector:
+                nc.vector.tensor_scalar(dst, src, half[:], None, ALU.mult)
+            else:
+                nc.scalar.activation(dst, src, ACT.Copy, scale=0.5)
 
         for c in range(N_CHUNKS):
             if c > 0:
                 o_bf = round_chunk(c)
             quantized.append(quantize_chunk(c, o_bf))
-            if c < N_CHUNKS - 1:
-                fill_b(c, 0, 2, 2 * c)
-            if c < N_CHUNKS - 2:
-                fill_b(c, 2, 2, 2 * c + 1)
-        fill_b(3, 0, 1, 6)
-        fill_b(3, 1, 1, 7)
-        fill_b(3, 2, 2, 5)
-        rc_row = keep.tile([P, I], F32, name="rc_row", tag="o_raw%d" % (N_CHUNKS - 1), align_bytes=64)
-        nc.vector.tensor_copy(rc_row[:], rc_pool[:].indirect(idx[:]))
+            if c < 3:
+                fill_b(2 * c, (0, 1), (c,), False)
+            if c < 2:
+                fill_b(2 * c + 1, (2, 3), (c,), False)
+        half = keep.tile([P, 1], F32, name="half", tag="o_raw%d" % (N_CHUNKS - 1), align_bytes=64)
+        nc.vector.memset(half[:], 0.5)
+        fill_b(5, (2, 3), (2,), True)
+        fill_b(6, (0, 1), (3,), False)
+        fill_b(7, (2, 3), (3,), True)
 
-        turned = psum.tile([P, PACK, P], F32, name="turned", tag="bank4")
-        for g in range(PACK):
-            nc.tensor.transpose(turned[:, g, :], rc_row[:, g * P : (g + 1) * P], ident[:])
-        rc_col = keep.tile([P, PACK], F32, name="rc_col")
-        nc.scalar.copy(rc_col[:], turned[:, :, RC_ROW])
-        spread = psum.tile([P, PACK, P], F32, name="spread", tag="bank7")
-        for g in range(PACK):
-            nc.tensor.transpose(spread[:, g, :], rc_col[:, g : g + 1].to_broadcast([P, P]), ident[:])
-        fill_b(2, 2, 2, 6)
+        cand_w = keep.tile([P, I], U32, name="cand_w", align_bytes=64)
+        for h in range(2):
+            nc.vector.tensor_copy(
+                cand_w[:, h * HALF : (h + 1) * HALF],
+                word_pool[:].bitcast(U32).indirect(idx[:, h * HALF // 16 : (h + 1) * HALF // 16]),
+            )
 
-        rc_all = keep.tile([P, I], F32, name="rc_all", align_bytes=64)
-        nc.scalar.copy(rc_all[:], spread[:].rearrange("p g i -> p (g i)"))
+        means = {}
+        picked = [keep.tile([P, J], F32, name="picked_b%d" % t, align_bytes=64) for t in range(PACK)]
 
-        means = []
-        for t in range(PACK):
-            if t == 2:
-                cand_w = keep.tile([P, I], U32, name="cand_w", align_bytes=64)
-                nc.vector.tensor_copy(cand_w[:], word_pool[:].bitcast(U32).indirect(idx[:]))
-            picked_b = keep.tile([P, J], F32, name="picked_b%d" % t, align_bytes=64)
-            nc.vector.tensor_copy(picked_b[:], b_sb[t // 2][:, t % 2, :].indirect(idx2[:]))
+        def sum_up(t):
             shares = keep.tile([P, J], F32, name="shares%d" % t, align_bytes=64)
             mean = keep.tile([P, 1], F32, name="mean%d" % t)
-            nc.scalar.activation(shares[:], picked_b[:], ACT.Copy, scale=1.0 / J, accum_out=mean[:])
-            means.append(mean)
+            nc.scalar.activation(shares[:], picked[t][:], ACT.Copy, scale=1.0 / J, accum_out=mean[:])
+            means[t] = mean
+
+        for t in range(2):
+            nc.scalar.activation(picked[t][:], b_sb[:, t, :].indirect(idx2[:]), ACT.Copy)
+            sum_up(t)
+        nc.vector.tensor_copy(picked[3][:], b_sb[:, 3, :].indirect(idx2[:]))
+        nc.vector.tensor_copy(picked[2][:, : J // 2], b_sb[:, 2, :].indirect(idx2[:, : J // 32]))
+        nc.scalar.activation(picked[2][:, J // 2 :], b_sb[:, 2, :].indirect(idx2[:, J // 32 :]), ACT.Copy)
+        sum_up(3)
+        sum_up(2)
 
         y_w = keep.tile([P, I], I32, name="y_w", align_bytes=64)
         y_s = keep.tile([P, I], U8, name="y_s", align_bytes=64)
         out_rows = out_0.rearrange("(p t) i -> p t i", t=PACK)
         out_words = out_1[0].rearrange("p n t -> p (n t)").bitcast(I32)
-        banks_a = {}
-        for h in range(2):
+        ys = [keep.tile([P, PACK, HALF], F32, name="y%d" % h, align_bytes=64) for h in range(2)]
+        order = [(h, t) for h in range(2) for t in (0, 1, 3, 2)]
+        banks_a = []
+        for n, (h, t) in enumerate(order):
             cols = slice(h * HALF, (h + 1) * HALF)
-            for t in range(PACK):
-                bank = psum.tile([P, HALF], F32, name="bank_a%d_%d" % (h, t), tag="bank%d" % A_BANKS[PACK * h + t])
-                product(bank[:], t, cand_w[:, cols], cand_s[:, cols])
-                banks_a[(h, t)] = bank
+            bank = psum.tile([P, HALF], F32, name="bank_a%d_%d" % (h, t), tag="bank%d" % n)
+            product(bank[:], t, cand_w[:, cols], cand_s[:, cols])
+            banks_a.append(bank)
 
-        for h in range(2):
-            cols = slice(h * HALF, (h + 1) * HALF)
-            y = keep.tile([P, PACK, HALF], F32, name="y%d" % h, align_bytes=64)
-            for t in range(PACK):
-                nc.vector.scalar_tensor_tensor(
-                    y[:, t, :], banks_a[(h, t)][:], means[t][:], rc_all[:, cols], ALU.subtract, ALU.subtract
-                )
-                if t % 2 == 1:
-                    nc.sync.dma_start(out_rows[:, t - 1 : t + 1, cols], y[:, t - 1 : t + 1, :])
+        def finish(h):
             y_bf = keep.tile([P, HALF, PACK], BF16, name="y_bf%d" % h, align_bytes=64)
             dst = y_bf[:].rearrange("p (c i) t -> p c t i", i=RUN)
-            src = y[:].rearrange("p t (c i) -> p c t i", i=RUN)
+            src = ys[h][:].rearrange("p t (c i) -> p c t i", i=RUN)
             if h == 0:
                 nc.scalar.copy(dst, src)
-                parts = ((0, HALF),)
             else:
                 middle = HALF // RUN // 2
                 nc.vector.tensor_copy(dst[:, :middle], src[:, :middle])
                 nc.scalar.copy(dst[:, middle:], src[:, middle:])
-                parts = ((HALF // 2, HALF), (0, HALF // 2))
-            for lo, hi in parts:
+            return y_bf
+
+        rounded = {}
+        done = set()
+        for n, (h, t) in enumerate(order):
+            cols = slice(h * HALF, (h + 1) * HALF)
+            nc.vector.scalar_tensor_tensor(
+                ys[h][:, t, :], banks_a[n][:], means[t][:], rc_all[:, cols], ALU.subtract, ALU.subtract
+            )
+            done.add((h, t))
+            if (h, t ^ 1) in done:
+                pair = slice(t // 2 * 2, t // 2 * 2 + 2)
+                nc.sync.dma_start(out_rows[:, pair, cols], ys[h][:, pair, :])
+            if all((h, e) in done for e in range(PACK)):
+                rounded[h] = finish(h)
+        for h in range(2):
+            cols = slice(h * HALF, (h + 1) * HALF)
+            for lo, hi in ((0, HALF),) if h == 0 else ((0, HALF // 2), (HALF // 2, HALF)):
                 part = slice(h * HALF + lo, h * HALF + hi)
                 nc.vector.quantize_mx(
                     out=y_w[:, part].bitcast(FP8X4),
                     scales=y_s[:, part],
-                    in_=y_bf[:, lo:hi].rearrange("p c t -> p (c t)"),
+                    in_=rounded[h][:, lo:hi].rearrange("p c t -> p (c t)"),
                 )
             nc.sync.dma_start(out_words[:, cols], y_w[:, cols])
 

@@ -22,7 +22,8 @@ HALF = I // 2
 CHUNK = 256
 N_CHUNKS = U // CHUNK
 Q_SPLIT = 84
-SHARED = 2
+SHARED = 1
+RC_SPLIT = 1408
 RC_ROW = P - 1
 
 
@@ -52,7 +53,8 @@ def tile_attend_localscaling_pl_kernel(tc, query, cand_words, cand_scales, other
         lane = keep.tile([P, 32], F32, name="lane", align_bytes=64)
         nc.vector.memset(ident[:], 0.0)
         nc.vector.tensor_tensor_scan(ramp[:], ones[:], ones[:], 0.0, ALU.mult, ALU.add)
-        nc.vector.memset(rc_pool[:RC_ROW, :].bitcast(I32), 0)
+        nc.vector.memset(rc_pool[:RC_ROW, :RC_SPLIT].bitcast(I32), 0)
+        nc.gpsimd.memset(rc_pool[:RC_ROW, RC_SPLIT:].bitcast(I32), 0)
         nc.vector.transpose(lane[:], ramp[:])
         nc.vector.memset(scale_pool[:].bitcast(I32), 0)
         for g in range(4):
@@ -78,12 +80,17 @@ def tile_attend_localscaling_pl_kernel(tc, query, cand_words, cand_scales, other
         nc.vector.tensor_copy(picked_s[:], scale_pool[:].indirect(idx[:]))
         cand_s = keep.tile([P, I], U8, name="cand_s", align_bytes=64)
         nc.vector.tensor_copy(cand_s[:].bitcast(I32), picked_s[:].bitcast(I32))
-        for g in range(1, 4):
+
+        def move_rows(g):
             nc.sync.dma_start(cand_s[32 * g : 32 * g + 4, :].bitcast(I32), picked_s[4 * g : 4 * g + 4, :].bitcast(I32))
+
+        move_rows(1)
+        move_rows(2)
         for c in range(3, N_CHUNKS):
             load_chunk(c)
         word_pool = keep.tile([P, T], I32, name="word_pool", align_bytes=64)
         nc.sync.dma_start(word_pool[:], cand_words[0].rearrange("p n t -> p (n t)").bitcast(I32))
+        move_rows(3)
 
         rc_row = keep.tile([P, I], F32, name="rc_row", align_bytes=64)
         nc.scalar.activation(rc_row[:], rc_pool[:].indirect(idx[:]), ACT.Copy)
@@ -155,7 +162,7 @@ def tile_attend_localscaling_pl_kernel(tc, query, cand_words, cand_scales, other
         quantized = []
 
         def fill_b(bank_number, tiles, chunks, on_vector):
-            bank = psum.tile([P, len(tiles), len(chunks), CHUNK], F32, name="bank_b%d" % bank_number, tag="bank%d" % bank_number)
+            bank = psum.tile([P, len(tiles), len(chunks), CHUNK], F32, name="bank_b%d_%d" % (tiles[0], chunks[0]), tag="bank%d" % bank_number)
             for e, t in enumerate(tiles):
                 for n, c in enumerate(chunks):
                     product(bank[:, e, n, :], t, quantized[c][0][:], quantized[c][1][:])
@@ -177,8 +184,9 @@ def tile_attend_localscaling_pl_kernel(tc, query, cand_words, cand_scales, other
         half = keep.tile([P, 1], F32, name="half", tag="o_raw%d" % (N_CHUNKS - 1), align_bytes=64)
         nc.vector.memset(half[:], 0.5)
         fill_b(5, (2, 3), (2,), True)
-        fill_b(6, (0, 1), (3,), False)
-        fill_b(7, (2, 3), (3,), True)
+        fill_b(6, (0,), (3,), False)
+        fill_b(7, (1,), (3,), True)
+        fill_b(0, (2, 3), (3,), True)
 
         cand_w = keep.tile([P, I], U32, name="cand_w", align_bytes=64)
         for h in range(2):
@@ -200,8 +208,7 @@ def tile_attend_localscaling_pl_kernel(tc, query, cand_words, cand_scales, other
             nc.scalar.activation(picked[t][:], b_sb[:, t, :].indirect(idx2[:]), ACT.Copy)
             sum_up(t)
         nc.vector.tensor_copy(picked[3][:], b_sb[:, 3, :].indirect(idx2[:]))
-        nc.vector.tensor_copy(picked[2][:, : J // 2], b_sb[:, 2, :].indirect(idx2[:, : J // 32]))
-        nc.scalar.activation(picked[2][:, J // 2 :], b_sb[:, 2, :].indirect(idx2[:, J // 32 :]), ACT.Copy)
+        nc.scalar.activation(picked[2][:], b_sb[:, 2, :].indirect(idx2[:]), ACT.Copy)
         sum_up(3)
         sum_up(2)
 
@@ -214,7 +221,7 @@ def tile_attend_localscaling_pl_kernel(tc, query, cand_words, cand_scales, other
         banks_a = []
         for n, (h, t) in enumerate(order):
             cols = slice(h * HALF, (h + 1) * HALF)
-            bank = psum.tile([P, HALF], F32, name="bank_a%d_%d" % (h, t), tag="bank%d" % n)
+            bank = psum.tile([P, HALF], F32, name="bank_a%d_%d" % (h, t), tag="bank%d" % ((n + 1) % 8))
             product(bank[:], t, cand_w[:, cols], cand_s[:, cols])
             banks_a.append(bank)
 
@@ -252,8 +259,10 @@ def tile_attend_localscaling_pl_kernel(tc, query, cand_words, cand_scales, other
                     scales=y_s[:, part],
                     in_=rounded[h][:, lo:hi].rearrange("p c t -> p (c t)"),
                 )
-            nc.sync.dma_start(out_words[:, cols], y_w[:, cols])
+            if h == 0:
+                nc.sync.dma_start(out_words[:, cols], y_w[:, cols])
 
         for r in range(4):
-            queue = nc.scalar if r % 2 == 0 else nc.sync
+            queue = nc.scalar if r > 0 else nc.sync
             queue.dma_start(out_2[0, r:16:4, :].bitcast(I32), y_s[r:P:32, :].bitcast(I32))
+        nc.sync.dma_start(out_words[:, HALF:], y_w[:, HALF:])

@@ -177,16 +177,22 @@ def tile_attend_localscaling_pl_kernel(tc, query, cand_words, cand_scales, other
             if c > 0:
                 o_bf = round_chunk(c)
             quantized.append(quantize_chunk(c, o_bf))
-            if c < 3:
-                fill_b(2 * c, (0, 1), (c,), False)
             if c < 2:
-                fill_b(2 * c + 1, (2, 3), (c,), False)
+                for t in range(PACK):
+                    fill_b(PACK * c + t, (t,), (c,), False)
+            elif c == 2:
+                fill_b(0, (0, 1), (c,), False)
         half = keep.tile([P, 1], F32, name="half", tag="o_raw%d" % (N_CHUNKS - 1), align_bytes=64)
-        nc.vector.memset(half[:], 0.5)
-        fill_b(5, (2, 3), (2,), True)
-        fill_b(6, (0,), (3,), False)
-        fill_b(7, (1,), (3,), True)
-        fill_b(0, (2, 3), (3,), True)
+        nc.gpsimd.memset(half[:], 0.5)
+        fill_b(1, (2, 3), (2,), True)
+        for n in range(2):
+            width = CHUNK // 2
+            cols = slice(n * width, (n + 1) * width)
+            bank = psum.tile([P, width], F32, name="bank_first%d" % n, tag="bank%d" % (2 + n))
+            product(bank[:], 0, quantized[3][0][:, cols], quantized[3][1][:, cols])
+            nc.scalar.activation(b_sb[:, 0, U - CHUNK + n * width : U - CHUNK + (n + 1) * width], bank[:], ACT.Copy, scale=0.5)
+        fill_b(4, (1,), (3,), True)
+        fill_b(5, (2, 3), (3,), True)
 
         cand_w = keep.tile([P, I], U32, name="cand_w", align_bytes=64)
         for h in range(2):
@@ -209,19 +215,19 @@ def tile_attend_localscaling_pl_kernel(tc, query, cand_words, cand_scales, other
             sum_up(t)
         nc.vector.tensor_copy(picked[3][:], b_sb[:, 3, :].indirect(idx2[:]))
         nc.scalar.activation(picked[2][:], b_sb[:, 2, :].indirect(idx2[:]), ACT.Copy)
-        sum_up(3)
         sum_up(2)
+        sum_up(3)
 
         y_w = keep.tile([P, I], I32, name="y_w", align_bytes=64)
         y_s = keep.tile([P, I], U8, name="y_s", align_bytes=64)
         out_rows = out_0.rearrange("(p t) i -> p t i", t=PACK)
         out_words = out_1[0].rearrange("p n t -> p (n t)").bitcast(I32)
         ys = [keep.tile([P, PACK, HALF], F32, name="y%d" % h, align_bytes=64) for h in range(2)]
-        order = [(h, t) for h in range(2) for t in (0, 1, 3, 2)]
+        order = [(h, t) for h in range(2) for t in range(PACK)]
         banks_a = []
         for n, (h, t) in enumerate(order):
             cols = slice(h * HALF, (h + 1) * HALF)
-            bank = psum.tile([P, HALF], F32, name="bank_a%d_%d" % (h, t), tag="bank%d" % ((n + 1) % 8))
+            bank = psum.tile([P, HALF], F32, name="bank_a%d_%d" % (h, t), tag="bank%d" % ((n + 6) % 8))
             product(bank[:], t, cand_w[:, cols], cand_s[:, cols])
             banks_a.append(bank)
 

@@ -194,6 +194,10 @@ def tile_attend_localscaling_pl_kernel(tc, query, cand_words, cand_scales, other
         fill_b(4, (1,), (3,), True)
         fill_b(5, (2, 3), (3,), True)
 
+        unread = psum.tile([P, 2, CHUNK], F32, name="unread", tag="bank5")
+        for e in range(2):
+            product(unread[:, e, :], e, quantized[3][0][:], quantized[3][1][:])
+
         cand_w = keep.tile([P, I], U32, name="cand_w", align_bytes=64)
         for h in range(2):
             nc.vector.tensor_copy(

@@ -176,14 +176,15 @@ def tile_attend_localscaling_pl_kernel(tc, query, cand_words, cand_scales, other
         for c in range(N_CHUNKS):
             if c > 0:
                 o_bf = round_chunk(c)
+            if c == N_CHUNKS - 1:
+                half = keep.tile([P, 1], F32, name="half", tag="o_raw%d" % c, align_bytes=64)
+                nc.vector.memset(half[:], 0.5)
             quantized.append(quantize_chunk(c, o_bf))
             if c < 2:
                 for t in range(PACK):
                     fill_b(PACK * c + t, (t,), (c,), False)
             elif c == 2:
                 fill_b(0, (0, 1), (c,), False)
-        half = keep.tile([P, 1], F32, name="half", tag="o_raw%d" % (N_CHUNKS - 1), align_bytes=64)
-        nc.gpsimd.memset(half[:], 0.5)
         fill_b(1, (2, 3), (2,), True)
         for n in range(2):
             width = CHUNK // 2
@@ -193,10 +194,6 @@ def tile_attend_localscaling_pl_kernel(tc, query, cand_words, cand_scales, other
             nc.scalar.activation(b_sb[:, 0, U - CHUNK + n * width : U - CHUNK + (n + 1) * width], bank[:], ACT.Copy, scale=0.5)
         fill_b(4, (1,), (3,), True)
         fill_b(5, (2, 3), (3,), True)
-
-        unread = psum.tile([P, 2, CHUNK], F32, name="unread", tag="bank5")
-        for e in range(2):
-            product(unread[:, e, :], e, quantized[3][0][:], quantized[3][1][:])
 
         cand_w = keep.tile([P, I], U32, name="cand_w", align_bytes=64)
         for h in range(2):
@@ -208,14 +205,16 @@ def tile_attend_localscaling_pl_kernel(tc, query, cand_words, cand_scales, other
         means = {}
         picked = [keep.tile([P, J], F32, name="picked_b%d" % t, align_bytes=64) for t in range(PACK)]
 
+        shares = keep.tile([P, PACK, J], F32, name="shares", tag="o_raw%d" % (N_CHUNKS - 1), align_bytes=64)
+
         def sum_up(t):
-            shares = keep.tile([P, J], F32, name="shares%d" % t, align_bytes=64)
             mean = keep.tile([P, 1], F32, name="mean%d" % t)
-            nc.scalar.activation(shares[:], picked[t][:], ACT.Copy, scale=1.0 / J, accum_out=mean[:])
+            nc.scalar.activation(shares[:, t, :], picked[t][:], ACT.Copy, scale=1.0 / J, accum_out=mean[:])
             means[t] = mean
 
         for t in range(2):
             nc.scalar.activation(picked[t][:], b_sb[:, t, :].indirect(idx2[:]), ACT.Copy)
+        for t in range(2):
             sum_up(t)
         nc.vector.tensor_copy(picked[3][:], b_sb[:, 3, :].indirect(idx2[:]))
         nc.scalar.activation(picked[2][:], b_sb[:, 2, :].indirect(idx2[:]), ACT.Copy)

@@ -23,6 +23,7 @@ CHUNK = 256
 N_CHUNKS = U // CHUNK
 Q_SPLIT = 84
 SHARED = 1
+Y_SPLIT = 192
 RC_SPLIT = 1408
 RC_ROW = P - 1
 
@@ -226,7 +227,7 @@ def tile_attend_localscaling_pl_kernel(tc, query, cand_words, cand_scales, other
         out_rows = out_0.rearrange("(p t) i -> p t i", t=PACK)
         out_words = out_1[0].rearrange("p n t -> p (n t)").bitcast(I32)
         ys = [keep.tile([P, PACK, HALF], F32, name="y%d" % h, align_bytes=64) for h in range(2)]
-        order = [(h, t) for h in range(2) for t in range(PACK)]
+        order = ((0, 0), (0, 1), (0, 2), (1, 0), (0, 3), (1, 1), (1, 2), (1, 3))
         banks_a = []
         for n, (h, t) in enumerate(order):
             cols = slice(h * HALF, (h + 1) * HALF)
@@ -241,7 +242,7 @@ def tile_attend_localscaling_pl_kernel(tc, query, cand_words, cand_scales, other
             if h == 0:
                 nc.scalar.copy(dst, src)
             else:
-                middle = HALF // RUN // 2
+                middle = Y_SPLIT // RUN
                 nc.vector.tensor_copy(dst[:, :middle], src[:, :middle])
                 nc.scalar.copy(dst[:, middle:], src[:, middle:])
             return y_bf
@@ -261,13 +262,9 @@ def tile_attend_localscaling_pl_kernel(tc, query, cand_words, cand_scales, other
                 rounded[h] = finish(h)
         for h in range(2):
             cols = slice(h * HALF, (h + 1) * HALF)
-            for lo, hi in ((0, HALF),) if h == 0 else ((0, HALF // 2), (HALF // 2, HALF)):
-                part = slice(h * HALF + lo, h * HALF + hi)
-                nc.vector.quantize_mx(
-                    out=y_w[:, part].bitcast(FP8X4),
-                    scales=y_s[:, part],
-                    in_=rounded[h][:, lo:hi].rearrange("p c t -> p (c t)"),
-                )
+            nc.vector.quantize_mx(
+                out=y_w[:, cols].bitcast(FP8X4), scales=y_s[:, cols], in_=rounded[h][:].rearrange("p c t -> p (c t)")
+            )
             if h == 0:
                 nc.sync.dma_start(out_words[:, cols], y_w[:, cols])
 

@@ -203,15 +203,13 @@ def tile_attend_localscaling_pl_kernel(tc, query, cand_words, cand_scales, other
                 word_pool[:].bitcast(U32).indirect(idx[:, h * HALF // 16 : (h + 1) * HALF // 16]),
             )
 
-        means = {}
+        means = keep.tile([P, PACK], F32, name="means", tag="o_raw%d" % (N_CHUNKS - 1), align_bytes=64)
         picked = [keep.tile([P, J], F32, name="picked_b%d" % t, align_bytes=64) for t in range(PACK)]
 
-        shares = keep.tile([P, PACK, J], F32, name="shares", tag="o_raw%d" % (N_CHUNKS - 1), align_bytes=64)
+        shares = keep.tile([P, PACK, J], F32, name="shares", align_bytes=64)
 
         def sum_up(t):
-            mean = keep.tile([P, 1], F32, name="mean%d" % t)
-            nc.scalar.activation(shares[:, t, :], picked[t][:], ACT.Copy, scale=1.0 / J, accum_out=mean[:])
-            means[t] = mean
+            nc.scalar.activation(shares[:, t, :], picked[t][:], ACT.Copy, scale=1.0 / J, accum_out=means[:, t : t + 1])
 
         for t in range(2):
             nc.scalar.activation(picked[t][:], b_sb[:, t, :].indirect(idx2[:]), ACT.Copy)
@@ -252,7 +250,7 @@ def tile_attend_localscaling_pl_kernel(tc, query, cand_words, cand_scales, other
         for n, (h, t) in enumerate(order):
             cols = slice(h * HALF, (h + 1) * HALF)
             nc.vector.scalar_tensor_tensor(
-                ys[h][:, t, :], banks_a[n][:], means[t][:], rc_all[:, cols], ALU.subtract, ALU.subtract
+                ys[h][:, t, :], banks_a[n][:], means[:, t : t + 1], rc_all[:, cols], ALU.subtract, ALU.subtract
             )
             done.add((h, t))
             if (h, t ^ 1) in done:

@@ -23,7 +23,6 @@ CHUNK = 256
 N_CHUNKS = U // CHUNK
 Q_SPLIT = 84
 SHARED = 1
-Y_SPLIT = 192
 RC_SPLIT = 1408
 RC_ROW = P - 1
 
@@ -77,7 +76,7 @@ def tile_attend_localscaling_pl_kernel(tc, query, cand_words, cand_scales, other
 
 
         nc.vector.tensor_copy(scale_pool[0:16, :].bitcast(I32), scale_rows[:])
-        picked_s = keep.tile([P, I], U8, name="picked_s", align_bytes=64)
+        picked_s = keep.tile([P, I], U8, name="picked_s", tag="picked_s", align_bytes=64)
         nc.vector.tensor_copy(picked_s[:], scale_pool[:].indirect(idx[:]))
         cand_s = keep.tile([P, I], U8, name="cand_s", align_bytes=64)
         nc.vector.tensor_copy(cand_s[:].bitcast(I32), picked_s[:].bitcast(I32))
@@ -162,17 +161,15 @@ def tile_attend_localscaling_pl_kernel(tc, query, cand_words, cand_scales, other
         b_sb = keep.tile([P, PACK, U], F32, name="b_sb", align_bytes=64)
         quantized = []
 
-        def fill_b(bank_number, tiles, chunks, on_vector):
-            bank = psum.tile([P, len(tiles), len(chunks), CHUNK], F32, name="bank_b%d_%d" % (tiles[0], chunks[0]), tag="bank%d" % bank_number)
+        def fill_b(bank_number, tiles, c, on_vector):
+            bank = psum.tile([P, len(tiles), CHUNK], F32, name="bank_b%d_%d" % (tiles[0], c), tag="bank%d" % bank_number)
             for e, t in enumerate(tiles):
-                for n, c in enumerate(chunks):
-                    product(bank[:, e, n, :], t, quantized[c][0][:], quantized[c][1][:])
-            dst = b_sb[:, tiles[0] : tiles[-1] + 1, chunks[0] * CHUNK : (chunks[-1] + 1) * CHUNK]
-            src = bank[:].rearrange("p e n c -> p e (n c)")
+                product(bank[:, e, :], t, quantized[c][0][:], quantized[c][1][:])
+            dst = b_sb[:, tiles[0] : tiles[-1] + 1, c * CHUNK : (c + 1) * CHUNK]
             if on_vector:
-                nc.vector.tensor_scalar(dst, src, half[:], None, ALU.mult)
+                nc.vector.tensor_scalar(dst, bank[:], half[:], None, ALU.mult)
             else:
-                nc.scalar.activation(dst, src, ACT.Copy, scale=0.5)
+                nc.scalar.activation(dst, bank[:], ACT.Copy, scale=0.5)
 
         for c in range(N_CHUNKS):
             if c > 0:
@@ -183,18 +180,20 @@ def tile_attend_localscaling_pl_kernel(tc, query, cand_words, cand_scales, other
             quantized.append(quantize_chunk(c, o_bf))
             if c < 2:
                 for t in range(PACK):
-                    fill_b(PACK * c + t, (t,), (c,), False)
+                    fill_b(PACK * c + t, (t,), c, False)
             elif c == 2:
-                fill_b(0, (0, 1), (c,), False)
-        fill_b(1, (2, 3), (2,), True)
-        for n in range(2):
-            width = CHUNK // 2
-            cols = slice(n * width, (n + 1) * width)
-            bank = psum.tile([P, width], F32, name="bank_first%d" % n, tag="bank%d" % (2 + n))
-            product(bank[:], 0, quantized[3][0][:, cols], quantized[3][1][:, cols])
-            nc.scalar.activation(b_sb[:, 0, U - CHUNK + n * width : U - CHUNK + (n + 1) * width], bank[:], ACT.Copy, scale=0.5)
-        fill_b(4, (1,), (3,), True)
-        fill_b(5, (2, 3), (3,), True)
+                fill_b(0, (0, 1), c, False)
+        fill_b(1, (2, 3), 2, True)
+        for t in (0, 2, 1, 3):
+            fill_b(2 + t, (t,), N_CHUNKS - 1, t >= 2)
+
+        means = keep.tile([P, PACK], F32, name="means", align_bytes=64)
+        tags = ["picked_s" if t == 2 else "picked_b%d" % t for t in range(PACK)]
+        picked = [keep.tile([P, J], F32, name="picked_b%d" % t, tag=tags[t], align_bytes=64) for t in range(PACK)]
+        shares = keep.tile([P, PACK, J], F32, name="shares", align_bytes=64)
+
+        def sum_up(t):
+            nc.scalar.activation(shares[:, t, :], picked[t][:], ACT.Copy, scale=1.0 / J, accum_out=means[:, t : t + 1])
 
         cand_w = keep.tile([P, I], U32, name="cand_w", align_bytes=64)
         for h in range(2):
@@ -202,71 +201,55 @@ def tile_attend_localscaling_pl_kernel(tc, query, cand_words, cand_scales, other
                 cand_w[:, h * HALF : (h + 1) * HALF],
                 word_pool[:].bitcast(U32).indirect(idx[:, h * HALF // 16 : (h + 1) * HALF // 16]),
             )
-
-        means = keep.tile([P, PACK], F32, name="means", tag="o_raw%d" % (N_CHUNKS - 1), align_bytes=64)
-        picked = [keep.tile([P, J], F32, name="picked_b%d" % t, align_bytes=64) for t in range(PACK)]
-
-        shares = keep.tile([P, PACK, J], F32, name="shares", align_bytes=64)
-
-        def sum_up(t):
-            nc.scalar.activation(shares[:, t, :], picked[t][:], ACT.Copy, scale=1.0 / J, accum_out=means[:, t : t + 1])
-
+        nc.vector.tensor_copy(picked[2][:], b_sb[:, 2, :].indirect(idx2[:]))
         for t in range(2):
             nc.scalar.activation(picked[t][:], b_sb[:, t, :].indirect(idx2[:]), ACT.Copy)
         for t in range(2):
             sum_up(t)
-        nc.vector.tensor_copy(picked[3][:], b_sb[:, 3, :].indirect(idx2[:]))
-        nc.scalar.activation(picked[2][:], b_sb[:, 2, :].indirect(idx2[:]), ACT.Copy)
-        sum_up(2)
-        sum_up(3)
+        nc.scalar.activation(picked[3][:], b_sb[:, 3, :].indirect(idx2[:]), ACT.Copy)
+        for t in range(2, PACK):
+            sum_up(t)
 
+        y = keep.tile([P, PACK, I], F32, name="y", align_bytes=64)
         y_w = keep.tile([P, I], I32, name="y_w", align_bytes=64)
         y_s = keep.tile([P, I], U8, name="y_s", align_bytes=64)
         out_rows = out_0.rearrange("(p t) i -> p t i", t=PACK)
         out_words = out_1[0].rearrange("p n t -> p (n t)").bitcast(I32)
-        ys = [keep.tile([P, PACK, HALF], F32, name="y%d" % h, align_bytes=64) for h in range(2)]
-        order = ((0, 0), (0, 1), (0, 2), (1, 0), (0, 3), (1, 1), (1, 2), (1, 3))
+        halves = (slice(0, HALF), slice(HALF, I))
+        pieces = [(t, cols) for cols in halves for t in range(2)] + [(t, cols) for t in range(2, PACK) for cols in halves]
         banks_a = []
-        for n, (h, t) in enumerate(order):
-            cols = slice(h * HALF, (h + 1) * HALF)
-            bank = psum.tile([P, HALF], F32, name="bank_a%d_%d" % (h, t), tag="bank%d" % ((n + 6) % 8))
+        for n, (t, cols) in enumerate(pieces):
+            bank = psum.tile([P, cols.stop - cols.start], F32, name="bank_a%d" % n, tag="bank%d" % ((n + 6) % 8))
             product(bank[:], t, cand_w[:, cols], cand_s[:, cols])
             banks_a.append(bank)
 
-        def finish(h):
-            y_bf = keep.tile([P, HALF, PACK], BF16, name="y_bf%d" % h, align_bytes=64)
-            dst = y_bf[:].rearrange("p (c i) t -> p c t i", i=RUN)
-            src = ys[h][:].rearrange("p t (c i) -> p c t i", i=RUN)
-            if h == 0:
-                nc.scalar.copy(dst, src)
-            else:
-                middle = Y_SPLIT // RUN
-                nc.vector.tensor_copy(dst[:, :middle], src[:, :middle])
-                nc.scalar.copy(dst[:, middle:], src[:, middle:])
+        def round_y(cols, engine_copy):
+            y_bf = keep.tile([P, cols.stop - cols.start, PACK], BF16, name="y_bf%d" % cols.start, align_bytes=64)
+            engine_copy(
+                y_bf[:].rearrange("p (c i) t -> p c t i", i=RUN), y[:, :, cols].rearrange("p t (c i) -> p c t i", i=RUN)
+            )
             return y_bf
 
-        rounded = {}
-        done = set()
-        for n, (h, t) in enumerate(order):
-            cols = slice(h * HALF, (h + 1) * HALF)
+        rounded = []
+        for n, (t, cols) in enumerate(pieces):
             nc.vector.scalar_tensor_tensor(
-                ys[h][:, t, :], banks_a[n][:], means[:, t : t + 1], rc_all[:, cols], ALU.subtract, ALU.subtract
+                y[:, t, cols], banks_a[n][:], means[:, t : t + 1], rc_all[:, cols], ALU.subtract, ALU.subtract
             )
-            done.add((h, t))
-            if (h, t ^ 1) in done:
-                pair = slice(t // 2 * 2, t // 2 * 2 + 2)
-                nc.sync.dma_start(out_rows[:, pair, cols], ys[h][:, pair, :])
-            if all((h, e) in done for e in range(PACK)):
-                rounded[h] = finish(h)
-        for h in range(2):
-            cols = slice(h * HALF, (h + 1) * HALF)
+            if t == 1:
+                nc.sync.dma_start(out_rows[:, 0:2, cols], y[:, 0:2, cols])
+            elif t > 1 and cols.stop == I:
+                nc.sync.dma_start(out_rows[:, t, :], y[:, t, :])
+            if t == PACK - 1:
+                rounded.append(round_y(cols, nc.scalar.copy if cols.start == 0 else nc.vector.tensor_copy))
+        for h in (1, 0):
+            cols = halves[h]
             nc.vector.quantize_mx(
                 out=y_w[:, cols].bitcast(FP8X4), scales=y_s[:, cols], in_=rounded[h][:].rearrange("p c t -> p (c t)")
             )
-            if h == 0:
+            if h == 1:
                 nc.sync.dma_start(out_words[:, cols], y_w[:, cols])
 
         for r in range(4):
             queue = nc.scalar if r > 0 else nc.sync
             queue.dma_start(out_2[0, r:16:4, :].bitcast(I32), y_s[r:P:32, :].bitcast(I32))
-        nc.sync.dma_start(out_words[:, HALF:], y_w[:, HALF:])
+        nc.sync.dma_start(out_words[:, :HALF], y_w[:, :HALF])

@@ -23,6 +23,7 @@ CHUNK = 256
 N_CHUNKS = U // CHUNK
 Q_SPLIT = 84
 SHARED = 1
+Y_SPLIT = 192
 RC_SPLIT = 1408
 RC_ROW = P - 1
 
@@ -216,18 +217,21 @@ def tile_attend_localscaling_pl_kernel(tc, query, cand_words, cand_scales, other
         out_rows = out_0.rearrange("(p t) i -> p t i", t=PACK)
         out_words = out_1[0].rearrange("p n t -> p (n t)").bitcast(I32)
         halves = (slice(0, HALF), slice(HALF, I))
-        pieces = [(t, cols) for cols in halves for t in range(2)] + [(t, cols) for t in range(2, PACK) for cols in halves]
+        pieces = [(t, cols) for pair in ((0, 1), (2, 3)) for cols in halves for t in pair]
         banks_a = []
         for n, (t, cols) in enumerate(pieces):
             bank = psum.tile([P, cols.stop - cols.start], F32, name="bank_a%d" % n, tag="bank%d" % ((n + 6) % 8))
             product(bank[:], t, cand_w[:, cols], cand_s[:, cols])
             banks_a.append(bank)
 
-        def round_y(cols, engine_copy):
-            y_bf = keep.tile([P, cols.stop - cols.start, PACK], BF16, name="y_bf%d" % cols.start, align_bytes=64)
-            engine_copy(
-                y_bf[:].rearrange("p (c i) t -> p c t i", i=RUN), y[:, :, cols].rearrange("p t (c i) -> p c t i", i=RUN)
-            )
+        def round_y(cols):
+            y_bf = keep.tile([P, HALF, PACK], BF16, name="y_bf%d" % cols.start, align_bytes=64)
+            dst = y_bf[:].rearrange("p (c i) t -> p c t i", i=RUN)
+            src = y[:, :, cols].rearrange("p t (c i) -> p c t i", i=RUN)
+            middle = (HALF // 2 if cols.start == 0 else Y_SPLIT) // RUN
+            copy = nc.scalar.copy if cols.start == 0 else nc.vector.tensor_copy
+            copy(dst[:, :middle], src[:, :middle])
+            nc.scalar.copy(dst[:, middle:], src[:, middle:])
             return y_bf
 
         rounded = []
@@ -235,21 +239,23 @@ def tile_attend_localscaling_pl_kernel(tc, query, cand_words, cand_scales, other
             nc.vector.scalar_tensor_tensor(
                 y[:, t, cols], banks_a[n][:], means[:, t : t + 1], rc_all[:, cols], ALU.subtract, ALU.subtract
             )
-            if t == 1:
-                nc.sync.dma_start(out_rows[:, 0:2, cols], y[:, 0:2, cols])
-            elif t > 1 and cols.stop == I:
-                nc.sync.dma_start(out_rows[:, t, :], y[:, t, :])
+            if t % 2 == 1:
+                nc.sync.dma_start(out_rows[:, t - 1 : t + 1, cols], y[:, t - 1 : t + 1, cols])
             if t == PACK - 1:
-                rounded.append(round_y(cols, nc.scalar.copy if cols.start == 0 else nc.vector.tensor_copy))
-        for h in (1, 0):
-            cols = halves[h]
-            nc.vector.quantize_mx(
-                out=y_w[:, cols].bitcast(FP8X4), scales=y_s[:, cols], in_=rounded[h][:].rearrange("p c t -> p (c t)")
-            )
-            if h == 1:
-                nc.sync.dma_start(out_words[:, cols], y_w[:, cols])
+                rounded.append(round_y(cols))
+        for h in range(2):
+            for n in range(2):
+                part = slice(n * HALF // 2, (n + 1) * HALF // 2)
+                cols = slice(h * HALF + part.start, h * HALF + part.stop)
+                nc.vector.quantize_mx(
+                    out=y_w[:, cols].bitcast(FP8X4),
+                    scales=y_s[:, cols],
+                    in_=rounded[h][:, part].rearrange("p c t -> p (c t)"),
+                )
+            if h == 0:
+                nc.sync.dma_start(out_words[:, :HALF], y_w[:, :HALF])
 
         for r in range(4):
             queue = nc.scalar if r > 0 else nc.sync
             queue.dma_start(out_2[0, r:16:4, :].bitcast(I32), y_s[r:P:32, :].bitcast(I32))
-        nc.sync.dma_start(out_words[:, :HALF], y_w[:, :HALF])
+        nc.sync.dma_start(out_words[:, HALF:], y_w[:, HALF:])

@@ -23,7 +23,8 @@ CHUNK = 256
 N_CHUNKS = U // CHUNK
 Q_SPLIT = 84
 SHARED = 1
-Y_SPLIT = 192
+Y_SPLIT = 96
+QUARTER = I // 4
 RC_SPLIT = 1408
 RC_ROW = P - 1
 
@@ -211,51 +212,53 @@ def tile_attend_localscaling_pl_kernel(tc, query, cand_words, cand_scales, other
         for t in range(2, PACK):
             sum_up(t)
 
-        y = keep.tile([P, PACK, I], F32, name="y", align_bytes=64)
+        ys = [keep.tile([P, PACK, HALF], F32, name="y%d" % h, align_bytes=64) for h in range(2)]
         y_w = keep.tile([P, I], I32, name="y_w", align_bytes=64)
         y_s = keep.tile([P, I], U8, name="y_s", align_bytes=64)
         out_rows = out_0.rearrange("(p t) i -> p t i", t=PACK)
         out_words = out_1[0].rearrange("p n t -> p (n t)").bitcast(I32)
         halves = (slice(0, HALF), slice(HALF, I))
-        pieces = [(t, cols) for pair in ((0, 1), (2, 3)) for cols in halves for t in pair]
+        pieces = [(t, cols) for cols in halves for t in (0, 1)] + [(t, cols) for cols in halves[::-1] for t in (2, 3)]
         banks_a = []
         for n, (t, cols) in enumerate(pieces):
             bank = psum.tile([P, cols.stop - cols.start], F32, name="bank_a%d" % n, tag="bank%d" % ((n + 6) % 8))
             product(bank[:], t, cand_w[:, cols], cand_s[:, cols])
             banks_a.append(bank)
 
-        def round_y(cols):
-            y_bf = keep.tile([P, HALF, PACK], BF16, name="y_bf%d" % cols.start, align_bytes=64)
-            dst = y_bf[:].rearrange("p (c i) t -> p c t i", i=RUN)
-            src = y[:, :, cols].rearrange("p t (c i) -> p c t i", i=RUN)
-            middle = (HALF // 2 if cols.start == 0 else Y_SPLIT) // RUN
-            copy = nc.scalar.copy if cols.start == 0 else nc.vector.tensor_copy
-            copy(dst[:, :middle], src[:, :middle])
-            nc.scalar.copy(dst[:, middle:], src[:, middle:])
-            return y_bf
+        rounded = [keep.tile([P, HALF, PACK], BF16, name="y_bf%d" % h, align_bytes=64) for h in range(2)]
 
-        rounded = []
+        def views(first, last, tiles):
+            h = first // HALF
+            cols = slice(first - h * HALF, last - h * HALF)
+            dst = rounded[h][:, cols, tiles].rearrange("p (c i) t -> p c t i", i=RUN)
+            return dst, ys[h][:, tiles, cols].rearrange("p t (c i) -> p c t i", i=RUN)
+
         for n, (t, cols) in enumerate(pieces):
             nc.vector.scalar_tensor_tensor(
-                y[:, t, cols], banks_a[n][:], means[:, t : t + 1], rc_all[:, cols], ALU.subtract, ALU.subtract
+                ys[cols.start // HALF][:, t, :], banks_a[n][:], means[:, t : t + 1], rc_all[:, cols], ALU.subtract, ALU.subtract
             )
             if t % 2 == 1:
-                nc.sync.dma_start(out_rows[:, t - 1 : t + 1, cols], y[:, t - 1 : t + 1, cols])
-            if t == PACK - 1:
-                rounded.append(round_y(cols))
-        for h in range(2):
-            for n in range(2):
-                part = slice(n * HALF // 2, (n + 1) * HALF // 2)
-                cols = slice(h * HALF + part.start, h * HALF + part.stop)
+                nc.sync.dma_start(out_rows[:, t - 1 : t + 1, cols], ys[cols.start // HALF][:, t - 1 : t + 1, :])
+            if (t, cols.start) == (1, 0):
+                pair = ys[0][:, 0:2, :].rearrange("p t c -> p c t")
+                nc.gpsimd.tensor_scalar(rounded[0][:, :, 0:2], pair, 1.0, 0.0, ALU.mult, ALU.add)
+            elif (t, cols.start) == (PACK - 1, HALF):
+                nc.scalar.copy(*views(HALF, HALF + Y_SPLIT, slice(0, PACK)))
+        nc.vector.tensor_copy(*views(HALF + Y_SPLIT, I, slice(0, PACK)))
+        for first in (0, QUARTER):
+            nc.scalar.copy(*views(first, first + QUARTER, slice(2, PACK)))
+        for h in (1, 0):
+            for first in (0, QUARTER):
+                cols = slice(h * HALF + first, h * HALF + first + QUARTER)
                 nc.vector.quantize_mx(
                     out=y_w[:, cols].bitcast(FP8X4),
                     scales=y_s[:, cols],
-                    in_=rounded[h][:, part].rearrange("p c t -> p (c t)"),
+                    in_=rounded[h][:, first : first + QUARTER].rearrange("p c t -> p (c t)"),
                 )
-            if h == 0:
-                nc.sync.dma_start(out_words[:, :HALF], y_w[:, :HALF])
+            if h == 1:
+                nc.sync.dma_start(out_words[:, HALF:], y_w[:, HALF:])
 
         for r in range(4):
             queue = nc.scalar if r > 0 else nc.sync
             queue.dma_start(out_2[0, r:16:4, :].bitcast(I32), y_s[r:P:32, :].bitcast(I32))
-        nc.sync.dma_start(out_words[:, HALF:], y_w[:, HALF:])
+        nc.sync.dma_start(out_words[:, :HALF], y_w[:, :HALF])

from contextlib import ExitStack

import concourse.mybir as mybir

D, T, I, U, J, Q = 512, 2048, 512, 1024, 256, 512
FLOPS = 2 * D * Q * (I + U)

F32 = mybir.dt.float32
BF16 = mybir.dt.bfloat16
I32 = mybir.dt.int32
U32 = mybir.dt.uint32
U16 = mybir.dt.uint16
U8 = mybir.dt.uint8
FP8X4 = mybir.dt.float8_e4m3fn_x4
ACT = mybir.ActivationFunctionType
ALU = mybir.AluOpType

P = 128
PACK = 4
RUN = 4
HALF = I // 2
CHUNK = 256
N_CHUNKS = U // CHUNK
Q_SPLIT = 84
SHARED = 1
Y_SPLIT = 96
QUARTER = I // 4
RC_SPLIT = 1408
RC_ROW = P - 1


def tile_attend_localscaling_pl_kernel(tc, query, cand_words, cand_scales, other, rc, offs, offs2, out_0, out_1, out_2):
    nc = tc.nc
    with ExitStack() as ctx:
        keep = ctx.enter_context(tc.tile_pool(name="keep", bufs=1))
        psum = ctx.enter_context(tc.psum_pool(name="psum", bufs=1))

        idx = keep.tile([P, I // 16], U16, name="idx")
        idx2 = keep.tile([P, J // 16], U16, name="idx2")
        nc.sync.dma_start(idx[:], offs)

        scale_pool = keep.tile([P, T], U8, name="scale_pool", align_bytes=64)
        rc_pool = keep.tile([P, T], F32, name="rc_pool", align_bytes=64)
        nc.scalar.dma_start(rc_pool[RC_ROW : RC_ROW + 1, :], rc[0:1, :])
        scale_rows = keep.tile([16, T // 4], I32, name="scale_rows", align_bytes=64)
        nc.sync.dma_start(scale_rows[:], cand_scales[0].bitcast(I32))

        ones = keep.tile([P, 32], F32, name="ones", align_bytes=64)
        two = keep.tile([P, 1], F32, name="two")
        nc.vector.memset(ones[:], 1.0)
        nc.scalar.activation(two[:], ones[:, 0:1], ACT.Copy, scale=2.0)

        ident = keep.tile([P, P], F32, name="ident")
        ramp = keep.tile([P, 32], F32, name="ramp", align_bytes=64)
        lane = keep.tile([P, 32], F32, name="lane", align_bytes=64)
        nc.vector.memset(ident[:], 0.0)
        nc.vector.tensor_tensor_scan(ramp[:], ones[:], ones[:], 0.0, ALU.mult, ALU.add)
        nc.vector.memset(rc_pool[:RC_ROW, :RC_SPLIT].bitcast(I32), 0)
        nc.gpsimd.memset(rc_pool[:RC_ROW, RC_SPLIT:].bitcast(I32), 0)
        nc.vector.transpose(lane[:], ramp[:])
        nc.vector.memset(scale_pool[:].bitcast(I32), 0)
        for g in range(4):
            rows = slice(32 * g, 32 * g + 32)
            nc.vector.tensor_tensor(ident[rows, rows], ramp[rows, :], lane[rows, :], ALU.is_equal)

        q_raw = keep.tile([P, PACK, Q], F32, name="q_raw", tag="q_raw", align_bytes=64)
        nc.sync.dma_start(q_raw[:], query.rearrange("(p j) c -> p j c", j=PACK))
        o_raws = []

        def load_chunk(c):
            o_raw = keep.tile([P, PACK, CHUNK], F32, name="o_raw%d" % c, align_bytes=64)
            nc.sync.dma_start(o_raw[:], other[:, c * CHUNK : (c + 1) * CHUNK].rearrange("(p j) c -> p j c", j=PACK))
            o_raws.append(o_raw)

        for c in range(3):
            load_chunk(c)
        nc.sync.dma_start(idx2[:], offs2)


        nc.vector.tensor_copy(scale_pool[0:16, :].bitcast(I32), scale_rows[:])
        picked_s = keep.tile([P, I], U8, name="picked_s", tag="picked_s", align_bytes=64)
        nc.vector.tensor_copy(picked_s[:], scale_pool[:].indirect(idx[:]))
        cand_s = keep.tile([P, I], U8, name="cand_s", align_bytes=64)
        nc.vector.tensor_copy(cand_s[:].bitcast(I32), picked_s[:].bitcast(I32))

        def move_rows(g):
            nc.sync.dma_start(cand_s[32 * g : 32 * g + 4, :].bitcast(I32), picked_s[4 * g : 4 * g + 4, :].bitcast(I32))

        move_rows(1)
        move_rows(2)
        for c in range(3, N_CHUNKS):
            load_chunk(c)
        word_pool = keep.tile([P, T], I32, name="word_pool", align_bytes=64)
        nc.sync.dma_start(word_pool[:], cand_words[0].rearrange("p n t -> p (n t)").bitcast(I32))
        move_rows(3)

        rc_row = keep.tile([P, I], F32, name="rc_row", align_bytes=64)
        nc.scalar.activation(rc_row[:], rc_pool[:].indirect(idx[:]), ACT.Copy)
        turned = psum.tile([P, PACK, P], F32, name="turned", tag="bank6")
        for g in range(PACK):
            nc.tensor.transpose(turned[:, g, :], rc_row[:, g * P : (g + 1) * P], ident[:])

        q_bf = keep.tile([P, PACK, P, PACK], BF16, name="q_bf", align_bytes=64)
        q_dst = q_bf[:].rearrange("p t m j -> p m j t")
        q_src = q_raw[:].rearrange("p j (m t) -> p m j t", t=PACK)
        for k in range(2):
            pair = slice(2 * k, 2 * k + 2)
            nc.vector.tensor_scalar(q_dst[:, :Q_SPLIT, :, pair], q_src[:, :Q_SPLIT, :, pair], 2.0, None, ALU.mult)
        nc.scalar.activation(q_dst[:, Q_SPLIT:], q_src[:, Q_SPLIT:], ACT.Copy, scale=two[:])

        rc_col = keep.tile([P, PACK], F32, name="rc_col")
        nc.scalar.copy(rc_col[:], turned[:, :, RC_ROW])
        spread = psum.tile([P, PACK, P], F32, name="spread", tag="bank7")
        for g in range(PACK):
            nc.tensor.transpose(spread[:, g, :], rc_col[:, g : g + 1].to_broadcast([P, P]), ident[:])

        def round_chunk(c):
            o_bf = keep.tile([P, CHUNK, PACK], BF16, name="o_bf%d" % c, align_bytes=64)
            dst = o_bf[:].rearrange("p (c i) j -> p c j i", i=RUN)
            src = o_raws[c][:].rearrange("p j (c i) -> p c j i", i=RUN)
            middle = CHUNK // RUN // 2
            nc.vector.tensor_copy(dst[:, :middle], src[:, :middle])
            if c < SHARED:
                nc.scalar.copy(dst[:, middle:], src[:, middle:])
            else:
                nc.vector.tensor_copy(dst[:, middle:], src[:, middle:])
            return o_bf

        def quantize_chunk(c, o_bf):
            o_w = keep.tile([P, CHUNK], U32, name="o_w%d" % c, align_bytes=64)
            o_s = keep.tile([P, CHUNK], U8, name="o_s%d" % c, align_bytes=64)
            for n in ((1, 0) if c < SHARED else (0, 1)):
                cols = slice(n * CHUNK // 2, (n + 1) * CHUNK // 2)
                nc.vector.quantize_mx(
                    out=o_w[:, cols].bitcast(FP8X4), scales=o_s[:, cols], in_=o_bf[:, cols].rearrange("p c j -> p (c j)")
                )
            return o_w, o_s

        o_bf = round_chunk(0)
        q_w = keep.tile([P, Q], U32, name="q_w", align_bytes=64)
        q_s = keep.tile([P, Q], U8, name="q_s", align_bytes=64)
        for t in range(PACK):
            cols = slice(t * P, (t + 1) * P)
            nc.vector.quantize_mx(
                out=q_w[:, cols].bitcast(FP8X4), scales=q_s[:, cols], in_=q_bf[:, t].rearrange("p m j -> p (m j)")
            )

        rc_all = keep.tile([P, I], F32, name="rc_all", align_bytes=64)
        nc.scalar.copy(rc_all[:], spread[:].rearrange("p g i -> p (g i)"))

        def product(out, t, words, scales):
            cols = slice(t * P, (t + 1) * P)
            nc.tensor.matmul_mx(
                out=out,
                lhsT=q_w[:, cols].bitcast(FP8X4),
                lhsT_scale=q_s[:, cols],
                rhs=words.bitcast(FP8X4),
                rhs_scale=scales,
                start=True,
                stop=True,
            )

        b_sb = keep.tile([P, PACK, U], F32, name="b_sb", align_bytes=64)
        quantized = []

        def fill_b(bank_number, tiles, c, on_vector):
            bank = psum.tile([P, len(tiles), CHUNK], F32, name="bank_b%d_%d" % (tiles[0], c), tag="bank%d" % bank_number)
            for e, t in enumerate(tiles):
                product(bank[:, e, :], t, quantized[c][0][:], quantized[c][1][:])
            dst = b_sb[:, tiles[0] : tiles[-1] + 1, c * CHUNK : (c + 1) * CHUNK]
            if on_vector:
                nc.vector.tensor_scalar(dst, bank[:], half[:], None, ALU.mult)
            else:
                nc.scalar.activation(dst, bank[:], ACT.Copy, scale=0.5)

        for c in range(N_CHUNKS):
            if c > 0:
                o_bf = round_chunk(c)
            if c == N_CHUNKS - 1:
                half = keep.tile([P, 1], F32, name="half", tag="o_raw%d" % c, align_bytes=64)
                nc.vector.memset(half[:], 0.5)
            quantized.append(quantize_chunk(c, o_bf))
            if c < 2:
                for t in range(PACK):
                    fill_b(PACK * c + t, (t,), c, False)
            elif c == 2:
                fill_b(0, (0, 1), c, False)
        fill_b(1, (2, 3), 2, True)
        for t in (0, 2, 1, 3):
            fill_b(2 + t, (t,), N_CHUNKS - 1, t >= 2)

        means = keep.tile([P, PACK], F32, name="means", align_bytes=64)
        tags = ["picked_s" if t == 2 else "picked_b%d" % t for t in range(PACK)]
        picked = [keep.tile([P, J], F32, name="picked_b%d" % t, tag=tags[t], align_bytes=64) for t in range(PACK)]
        shares = keep.tile([P, PACK, J], F32, name="shares", align_bytes=64)

        def sum_up(t):
            nc.scalar.activation(shares[:, t, :], picked[t][:], ACT.Copy, scale=1.0 / J, accum_out=means[:, t : t + 1])

        cand_w = keep.tile([P, I], U32, name="cand_w", align_bytes=64)
        for h in range(2):
            nc.vector.tensor_copy(
                cand_w[:, h * HALF : (h + 1) * HALF],
                word_pool[:].bitcast(U32).indirect(idx[:, h * HALF // 16 : (h + 1) * HALF // 16]),
            )
        nc.vector.tensor_copy(picked[2][:], b_sb[:, 2, :].indirect(idx2[:]))
        for t in range(2):
            nc.scalar.activation(picked[t][:], b_sb[:, t, :].indirect(idx2[:]), ACT.Copy)
        for t in range(2):
            sum_up(t)
        nc.scalar.activation(picked[3][:], b_sb[:, 3, :].indirect(idx2[:]), ACT.Copy)
        for t in range(2, PACK):
            sum_up(t)

        ys = [keep.tile([P, PACK, HALF], F32, name="y%d" % h, align_bytes=64) for h in range(2)]
        y_w = keep.tile([P, I], I32, name="y_w", align_bytes=64)
        y_s = keep.tile([P, I], U8, name="y_s", align_bytes=64)
        out_rows = out_0.rearrange("(p t) i -> p t i", t=PACK)
        out_words = out_1[0].rearrange("p n t -> p (n t)").bitcast(I32)
        halves = (slice(0, HALF), slice(HALF, I))
        pieces = [(t, cols) for cols in halves for t in (0, 1)] + [(t, cols) for cols in halves[::-1] for t in (2, 3)]
        banks_a = []
        for n, (t, cols) in enumerate(pieces):
            bank = psum.tile([P, cols.stop - cols.start], F32, name="bank_a%d" % n, tag="bank%d" % ((n + 6) % 8))
            product(bank[:], t, cand_w[:, cols], cand_s[:, cols])
            banks_a.append(bank)

        rounded = [keep.tile([P, HALF, PACK], BF16, name="y_bf%d" % h, align_bytes=64) for h in range(2)]

        def views(first, last, tiles):
            h = first // HALF
            cols = slice(first - h * HALF, last - h * HALF)
            dst = rounded[h][:, cols, tiles].rearrange("p (c i) t -> p c t i", i=RUN)
            return dst, ys[h][:, tiles, cols].rearrange("p t (c i) -> p c t i", i=RUN)

        for n, (t, cols) in enumerate(pieces):
            nc.vector.scalar_tensor_tensor(
                ys[cols.start // HALF][:, t, :], banks_a[n][:], means[:, t : t + 1], rc_all[:, cols], ALU.subtract, ALU.subtract
            )
            if t % 2 == 1:
                nc.sync.dma_start(out_rows[:, t - 1 : t + 1, cols], ys[cols.start // HALF][:, t - 1 : t + 1, :])
            if (t, cols.start) == (1, 0):
                pair = ys[0][:, 0:2, :].rearrange("p t c -> p c t")
                nc.gpsimd.tensor_scalar(rounded[0][:, :, 0:2], pair, 1.0, 0.0, ALU.mult, ALU.add)
            elif (t, cols.start) == (PACK - 1, HALF):
                nc.scalar.copy(*views(HALF, HALF + Y_SPLIT, slice(0, PACK)))
        nc.vector.tensor_copy(*views(HALF + Y_SPLIT, I, slice(0, PACK)))
        for first in (0, QUARTER):
            nc.scalar.copy(*views(first, first + QUARTER, slice(2, PACK)))
        for h in (1, 0):
            for first in (0, QUARTER):
                cols = slice(h * HALF + first, h * HALF + first + QUARTER)
                nc.vector.quantize_mx(
                    out=y_w[:, cols].bitcast(FP8X4),
                    scales=y_s[:, cols],
                    in_=rounded[h][:, first : first + QUARTER].rearrange("p c t -> p (c t)"),
                )
            if h == 1:
                nc.sync.dma_start(out_words[:, HALF:], y_w[:, HALF:])

        for r in range(4):
            queue = nc.scalar if r > 0 else nc.sync
            queue.dma_start(out_2[0, r:16:4, :].bitcast(I32), y_s[r:P:32, :].bitcast(I32))
        nc.sync.dma_start(out_words[:, :HALF], y_w[:, :HALF])
